import numpy as np
import ml_dtypes


def mxq(x, axis, fmt="e4m3"):
    dtype, down = {"e4m3": (ml_dtypes.float8_e4m3fn, 7), "e5m2": (ml_dtypes.float8_e5m2, 14)}[fmt]
    v = np.moveaxis(np.asarray(x, np.float32).astype(ml_dtypes.bfloat16).astype(np.float64), axis, -1)
    blocks = v.reshape(v.shape[:-1] + (-1, 32))
    amax = np.abs(blocks).max(-1, keepdims=True)
    byte = np.maximum(np.where(amax > 0, np.frexp(amax)[1] - 1 + 127, 0) - down, 1)
    scale = np.exp2(byte - 127.0)
    codes = (blocks / scale).astype(np.float32).astype(dtype).astype(np.float64)
    return np.moveaxis((codes * scale).reshape(v.shape), -1, axis)


WIDE = False


def mx_kscale(k):
    if not WIDE:
        return np.ones(k)
    levels = np.array([10, -10, 5, -5, 0])
    if k % 512:
        return np.exp2(np.random.permutation(np.resize(levels, k // 32))).repeat(32)
    a = np.empty((k // 512, 16))
    for p in range(k // 512):
        a[p, :8] = np.random.permutation(np.resize(levels, 8))
        for g in range(8):
            far = levels[np.abs(levels - a[p, g]) >= 10]
            a[p, g + 8] = far[np.random.randint(len(far))]
    return np.exp2(a.ravel()).repeat(32)


BF16 = ml_dtypes.bfloat16


def bf(x):
    return np.asarray(x, np.float32).astype(BF16)


def f64(x):
    return np.asarray(x).astype(np.float64)


E2M1 = np.array([0.0, 0.5, 1.0, 1.5, 2.0, 3.0, 4.0, 6.0, -0.0, -0.5, -1.0, -1.5, -2.0, -3.0, -4.0, -6.0])


def pack_weight(w, fmt):
    k, n = w.shape
    w = f64(bf(w)).reshape(k // 32, 32, n)
    amax = np.abs(w).max(1)
    if fmt == "e4m3":
        byte = np.frexp(amax)[1] - 1 + 127 - 7
    else:
        mant, ex = np.frexp(amax / 6.0)
        byte = np.where(mant > 0.5, ex, ex - 1) + 127
    byte = np.clip(np.where(amax > 0, byte, 1), 1, 254)
    scaled = (w * np.exp2(127.0 - byte)[:, None, :]).reshape(k, n).astype(np.float32)
    by_word = np.ascontiguousarray(scaled.reshape(k // 512, 128, 4, n).transpose(0, 1, 3, 2))
    if fmt == "e4m3":
        words = by_word.astype(ml_dtypes.float8_e4m3fn).view(np.uint8)
    else:
        c = by_word.astype(ml_dtypes.float4_e2m1fn).view(np.uint8) & 0xF
        words = c[..., 0::2] | (c[..., 1::2] << 4)
    return np.ascontiguousarray(words), np.ascontiguousarray(byte.astype(np.uint8).reshape(k // 512, 16, n))


def unpack_weight(words, scales, fmt):
    g, p, n, _ = words.shape
    if fmt == "e4m3":
        vals = np.ascontiguousarray(words).view(ml_dtypes.float8_e4m3fn).astype(np.float64)
    else:
        nib = np.empty((g, p, n, 4), np.uint8)
        nib[..., 0::2] = words & 0xF
        nib[..., 1::2] = words >> 4
        vals = E2M1[nib]
    vals = vals * np.repeat(np.exp2(scales.astype(np.float64) - 127.0), 8, axis=1)[..., None]
    return vals.transpose(0, 1, 3, 2).reshape(g * 512, n)
def pack4(w):
    words, scales = pack_weight(w, "e2m1")
    return words.reshape(words.shape[0], 128, -1), scales


def unpack4(words, scales):
    return unpack_weight(words.reshape(words.shape[0], 128, -1, 2), scales, "e2m1")


def planes(Y):
    n, m = Y.shape
    b = f64(bf(Y)).reshape(n // 32, 32, m)
    amax = np.abs(b).max(1)
    byte = np.clip(np.where(amax > 0, np.frexp(amax)[1] - 1 + 127 - 7, 1), 1, 254)
    codes = (b * np.exp2(127.0 - byte)[:, None, :]).reshape(n, m).astype(np.float32).astype(ml_dtypes.float8_e4m3fn).view(np.uint8)
    words = codes.reshape(n // 512, 128, 4, m).transpose(0, 1, 3, 2)
    return np.ascontiguousarray(words), np.ascontiguousarray(byte.astype(np.uint8).reshape(n // 512, 16, m))


R, K, J, M = 768, 1024, 2048, 1536

def setup_inputs():
    s = mx_kscale(K)
    t = mx_kscale(J)
    marker_weight = 1.3 * np.exp(0.2 * np.random.randn(K, 1)) / np.sqrt(K)
    calls = marker_weight * np.tanh(2.0 * np.random.randn(K, R))
    panel = np.tanh(2.0 * np.random.randn(K, J))
    alleles = np.tanh(2.0 * np.random.randn(J, M))
    c_words, c_scales = pack4(calls * s[:, None])
    h_words, h_scales = pack4(panel / s[:, None])
    return {
        "c_words": c_words, "c_scales": c_scales,
        "h_words": h_words, "h_scales": h_scales,
        "hap_weight": bf(np.exp(0.3 * np.random.randn(J)) / np.sqrt(J) * t),
        "alleles": bf(alleles / t[:, None]),
        "target_scale": bf(np.exp(0.3 * np.random.randn(R))),
        "marker_gain": bf(np.exp(0.8 * np.random.randn(M))),
        "base": bf(0.3 * np.random.randn(M)),
    }

def reference(c_words, c_scales, h_words, h_scales, hap_weight, alleles, target_scale, marker_gain, base):
    C = unpack4(c_words, c_scales)
    H = unpack4(h_words, h_scales)
    S = C.T @ H
    E = np.exp(S) * f64(hap_weight)[None, :]
    D = mxq(E, 1, "e4m3") @ mxq(f64(alleles), 0, "e4m3")
    y = D * f64(target_scale)[:, None] * f64(marker_gain)[None, :] + f64(base)[None, :]
    Y = y.T
    words, scales = planes(Y)
    return y, words, scales

@@ -1,0 +1,330 @@
+from contextlib import ExitStack
+
+import concourse.mybir as mybir
+from concourse.masks import make_identity
+
+R, K, J, M = 768, 1024, 2048, 1536
+FLOPS = 2 * R * K * J + 2 * R * J * M
+
+F32 = mybir.dt.float32
+BF16 = mybir.dt.bfloat16
+I32 = mybir.dt.int32
+U32 = mybir.dt.uint32
+U8 = mybir.dt.uint8
+FP8X4 = mybir.dt.float8_e4m3fn_x4
+FP4X4 = mybir.dt.float4_e2m1fn_x4
+ACT = mybir.ActivationFunctionType
+ALU = mybir.AluOpType
+
+P = 128
+PASS = 512
+K_PASSES = K // PASS
+J_PASSES = J // PASS
+M_CHUNKS = M // PASS
+R_TILES = R // P
+R_CHUNKS = ((0, 512), (512, 256))
+TS_ROW = 32
+
+
+def tile_haplotype_emission_alleles_k5_kernel(
+    tc, c_words, c_scales, h_words, h_scales, hap_weight, alleles, target_scale, marker_gain, base, out_0, out_1, out_2
+):
+    nc = tc.nc
+    with ExitStack() as ctx:
+        keep = ctx.enter_context(tc.tile_pool(name="keep", bufs=1))
+        work = ctx.enter_context(tc.tile_pool(name="work", bufs=1))
+        psum = ctx.enter_context(tc.psum_pool(name="psum", bufs=1))
+        ctx.enter_context(tc.manual_schedule())
+
+        def kept(name, shape, dtype):
+            return keep.tile(shape, dtype, name=name, align_bytes=64)
+
+        ident = kept("ident", [P, P], F32)
+        rows_bf = kept("rows_bf", [P, PASS], BF16)
+        rows = kept("rows", [P, 4, P], F32)
+        ln_w = kept("ln_w", [P, 4, J_PASSES], F32)
+        ts_col = kept("ts_col", [P, R_TILES], F32)
+        warm = kept("warm", [P, 2], F32)
+        gain_bc = kept("gain_bc", [P, M], BF16)
+        base_bc = kept("base_bc", [P, M], BF16)
+        c_codes = [kept("c_codes%d" % c, [P, K_PASSES, 2 * R_CHUNKS[c][1]], U8) for c in range(2)]
+        c_plane = kept("c_plane", [P, K_PASSES, R], U8)
+        h_plane_raw = kept("h_plane_raw", [P, K_PASSES, J], U8)
+        h_raw = [kept("h_raw%d" % a, [P, K_PASSES, 2 * PASS], U8) for a in range(J_PASSES)]
+        h_codes = [kept("h_codes%d" % a, [P, K_PASSES, 4, 2 * P], U8) for a in range(J_PASSES)]
+        h_plane = [kept("h_plane%d" % a, [P, K_PASSES, 4, P], U8) for a in range(J_PASSES)]
+        a_first = [kept("a_first%d" % a, [P, 4, PASS], BF16) for a in range(J_PASSES)]
+        a_rest = [kept("a_rest%d" % a, [P, 4, M - PASS], BF16) for a in range(J_PASSES)]
+        a_codes = {(a, g): kept("a_codes%d_%d" % (a, g), [P, PASS], U32) for a in range(J_PASSES) for g in range(M_CHUNKS)}
+        a_plane = {(a, g): kept("a_plane%d_%d" % (a, g), [P, PASS], U8) for a in range(J_PASSES) for g in range(M_CHUNKS)}
+        e_rows = {(a, c): kept("e_rows%d_%d" % (a, c), [P, 4, R_CHUNKS[c][1]], BF16) for a in range(J_PASSES) for c in range(2)}
+        e_codes = {(a, c): kept("e_codes%d_%d" % (a, c), [P, R_CHUNKS[c][1]], U32) for a in range(J_PASSES) for c in range(2)}
+        e_plane = {(a, c): kept("e_plane%d_%d" % (a, c), [P, R_CHUNKS[c][1]], U8) for a in range(J_PASSES) for c in range(2)}
+        y_plane = [kept("y_plane%d" % g, [P, R], U8) for g in range(M_CHUNKS)]
+
+        nc.vector.memset(warm[:], 1.0)
+        nc.vector.memset(h_plane_raw[:].rearrange("p g n -> p (g n)").bitcast(I32), 0)
+        nc.vector.memset(rows[:], 0.0)
+        nc.vector.memset(ident[:], 0.0)
+        nc.vector.memset(c_plane[:].rearrange("p g n -> p (g n)").bitcast(I32), 0)
+        nc.scalar.activation(out=warm[:, 1:2], in_=warm[:, 0:1], func=ACT.Ln)
+        make_identity(nc, ident[:], nomemset=True)
+
+        def load_plane(queue, plane, scales, quadrants):
+            for q in quadrants:
+                queue.dma_start(
+                    out=plane[32 * q : 32 * q + 4, :, :].bitcast(I32),
+                    in_=scales[:, 4 * q : 4 * q + 4, :].rearrange("g r n -> r g n").bitcast(I32),
+                )
+
+        def load_alleles(dst, a, cols):
+            src = alleles[PASS * a : PASS * (a + 1), cols].rearrange("(s t i) m -> i s t m", t=4, i=4)
+            for i in range(4):
+                nc.sync.dma_start(out=dst[i:P:4, :, :], in_=src[i])
+
+        def load_h(a):
+            nc.sync.dma_start(
+                out=h_raw[a][:].bitcast(I32),
+                in_=h_words[:, :, 2 * PASS * a : 2 * PASS * (a + 1)].rearrange("g p n -> p g n").bitcast(I32),
+            )
+
+        def load_c(c):
+            r0, width = R_CHUNKS[c]
+            nc.sync.dma_start(
+                out=c_codes[c][:].bitcast(I32),
+                in_=c_words[:, :, 2 * r0 : 2 * (r0 + width)].rearrange("g p n -> p g n").bitcast(I32),
+            )
+
+        nc.sync.dma_start(out=rows_bf[0:J_PASSES, :], in_=hap_weight.rearrange("(a n) -> a n", n=PASS))
+        load_alleles(a_first[0], 0, slice(0, PASS))
+        load_plane(nc.sync, h_plane_raw, h_scales, (0,))
+        load_h(0)
+        load_c(0)
+        load_plane(nc.sync, h_plane_raw, h_scales, (1, 2, 3))
+        load_plane(nc.sync, c_plane, c_scales, (0, 1, 2, 3))
+        load_h(1)
+        load_alleles(a_first[1], 1, slice(0, PASS))
+        load_h(2)
+        load_h(3)
+        nc.sync.dma_start(out=rows_bf[TS_ROW : TS_ROW + R_TILES, 0:P], in_=target_scale.rearrange("(a n) -> a n", n=P))
+        load_alleles(a_first[2], 2, slice(0, PASS))
+        load_alleles(a_first[3], 3, slice(0, PASS))
+        load_c(1)
+        nc.sync.dma_start(out=gain_bc[:], in_=marker_gain.partition_broadcast(P))
+        nc.sync.dma_start(out=base_bc[:], in_=base.partition_broadcast(P))
+        for a in range(J_PASSES):
+            load_alleles(a_rest[a], a, slice(PASS, M))
+
+        grouped = {}
+
+        def interleave(engine, key, src):
+            width = src.shape[2]
+            tag = "by_scalar" if engine is nc.scalar else "by_vector"
+            dst = work.tile([P, width, 4], BF16, name=tag, tag=tag, bufs=4, align_bytes=64)
+            grouped[key] = dst
+            o = dst[:].rearrange("p (c i) t -> p c t i", i=4)
+            s = src.rearrange("p t (c i) -> p c t i", i=4)
+            if engine is nc.scalar:
+                nc.scalar.copy(out=o, in_=s)
+            else:
+                nc.vector.tensor_copy(out=o, in_=s)
+
+        def quantise(key, codes, plane):
+            nc.vector.quantize_mx(out=codes.bitcast(FP8X4), scales=plane, in_=grouped[key][:].rearrange("p c t -> p (c t)"))
+
+        def al(engine, a, g):
+            src = a_first[a][:] if g == 0 else a_rest[a][:, :, PASS * (g - 1) : PASS * g]
+            interleave(engine, ("a", a, g), src)
+
+        def qa(a, g):
+            quantise(("a", a, g), a_codes[a, g][:], a_plane[a, g][:])
+
+        def ei(a, c):
+            interleave(nc.vector, ("e", a, c), e_rows[a, c][:])
+
+        def qe(a, c):
+            quantise(("e", a, c), e_codes[a, c][:], e_plane[a, c][:])
+
+        def sort_h(a):
+            nc.vector.tensor_copy(
+                out=h_codes[a][:].bitcast(I32).rearrange("p g t (s e) -> p g t s e", e=2),
+                in_=h_raw[a][:].bitcast(I32).rearrange("p g (s t e) -> p g t s e", t=4, e=2),
+            )
+            nc.vector.tensor_copy(
+                out=h_plane[a][:].bitcast(I32),
+                in_=h_plane_raw[:, :, PASS * a : PASS * (a + 1)].bitcast(I32).rearrange("p g (s t) -> p g t s", t=4),
+            )
+
+        def emission(a, c):
+            r0, width = R_CHUNKS[c]
+            for t in range(4):
+                bank = psum.tile([P, PASS], F32, name="s_bank", tag="s_bank", bufs=3)
+                for g in range(K_PASSES):
+                    nc.tensor.matmul_mx(
+                        out=bank[:, 0:width],
+                        lhsT=h_codes[a][:, g, t, :].bitcast(FP4X4),
+                        lhsT_scale=h_plane[a][:, g, t, :],
+                        rhs=c_codes[c][:, g, :].bitcast(FP4X4),
+                        rhs_scale=c_plane[:, g, r0 : r0 + width],
+                        start=(g == 0),
+                        stop=(g == K_PASSES - 1),
+                    )
+                nc.scalar.activation(out=e_rows[a, c][:, t, :], in_=bank[:, 0:width], func=ACT.Exp, bias=ln_w[:, t, a : a + 1])
+
+        d_of, z_of, y_of, yb_of, tb_of, yg_of = {}, {}, {}, {}, {}, {}
+
+        def product(n):
+            g, rt = divmod(n, R_TILES)
+            c = 0 if rt < 4 else 1
+            cols = slice(P * rt - R_CHUNKS[c][0], P * (rt + 1) - R_CHUNKS[c][0])
+            bank = psum.tile([P, PASS], F32, name="d_bank", tag="d_bank", bufs=3)
+            for a in range(J_PASSES):
+                nc.tensor.matmul_mx(
+                    out=bank[:],
+                    lhsT=e_codes[a, c][:, cols].bitcast(FP8X4),
+                    lhsT_scale=e_plane[a, c][:, cols],
+                    rhs=a_codes[a, g][:].bitcast(FP8X4),
+                    rhs_scale=a_plane[a, g][:],
+                    start=(a == 0),
+                    stop=(a == J_PASSES - 1),
+                )
+            d_of[n] = bank
+
+        def scale_d(n):
+            g, rt = divmod(n, R_TILES)
+            bank = d_of[n]
+            z = work.tile([P, PASS], F32, name="z", tag="z", bufs=3)
+            z_of[n] = z
+            nc.vector.scalar_tensor_tensor(
+                out=z[:], in0=bank[:], scalar=ts_col[:, rt : rt + 1], in1=gain_bc[:, PASS * g : PASS * (g + 1)],
+                op0=ALU.mult, op1=ALU.mult,
+            )
+
+        def finish(n):
+            g, rt = divmod(n, R_TILES)
+            y = work.tile([P, PASS], F32, name="y", tag="y", bufs=8)
+            y_of[n] = y
+            nc.vector.tensor_tensor(out=y[:], in0=z_of[n][:], in1=base_bc[:, PASS * g : PASS * (g + 1)], op=ALU.add)
+            nc.sync.dma_start(out=out_0[P * rt : P * (rt + 1), PASS * g : PASS * (g + 1)], in_=y[:])
+
+        def round_y(n, engine):
+            yb = work.tile([P, 2, P, 2], BF16, name="yb", tag="yb", bufs=4, align_bytes=64)
+            yb_of[n] = yb
+            src = y_of[n][:].rearrange("r (p u e) -> r u p e", u=2, e=2)
+            if engine is nc.scalar:
+                nc.scalar.copy(out=yb[:], in_=src)
+            else:
+                nc.vector.tensor_copy(out=yb[:], in_=src)
+
+        def turn(pair):
+            bank = psum.tile([P, 2, 2, P], F32, name="t_bank", tag="t_bank", bufs=2)
+            tb_of[pair] = bank
+            for h in range(2):
+                words = yb_of[2 * pair + h][:].rearrange("r u p e -> r (u p e)").bitcast(F32)
+                for u in range(2):
+                    nc.tensor.transpose(bank[:, h, u, :], words[:, P * u : P * (u + 1)], ident[:])
+
+        def leave(pair):
+            yg = work.tile([P, 2 * P * 4], BF16, name="yg", tag="yg", bufs=3, align_bytes=64)
+            yg_of[pair] = yg
+            nc.scalar.copy(
+                out=yg[:].bitcast(F32).rearrange("p (h r u) -> p h r u", h=2, u=2),
+                in_=tb_of[pair][:].rearrange("p h u r -> p h r u"),
+            )
+
+        def planes(pair):
+            g, k = divmod(pair, R_TILES // 2)
+            cols = slice(2 * P * k, 2 * P * (k + 1))
+            codes = work.tile([P, 2 * P], U32, name="y_codes", tag="y_codes", bufs=3, align_bytes=64)
+            nc.vector.quantize_mx(out=codes[:].bitcast(FP8X4), scales=y_plane[g][:, cols], in_=yg_of[pair][:])
+            nc.sync.dma_start(out=out_1[g, :, cols, :].rearrange("p m t -> p (m t)").bitcast(I32), in_=codes[:].bitcast(I32))
+            if k == R_TILES // 2 - 1:
+                for q in range(4):
+                    nc.sync.dma_start(out=out_2[g, 4 * q : 4 * q + 4, :].bitcast(I32), in_=y_plane[g][32 * q : 32 * q + 4, :].bitcast(I32))
+
+        nc.scalar.activation(
+            out=rows[0:J_PASSES, :, :].rearrange("a t (s i) -> a t s i", i=4),
+            in_=rows_bf[0:J_PASSES, :].rearrange("a (s t i) -> a t s i", t=4, i=4),
+            func=ACT.Ln,
+        )
+        nc.scalar.activation(out=warm[:, 1:2], in_=warm[:, 0:1], func=ACT.Exp)
+        al(nc.vector, 0, 0)
+        col_bank = psum.tile([P, 4, P], F32, name="t_bank", tag="t_bank", bufs=2)
+        for t in range(4):
+            nc.tensor.transpose(col_bank[:, t, :], rows[:, t, :], ident[:])
+        nc.vector.tensor_copy(out=ln_w[:], in_=col_bank[:, :, 0:J_PASSES])
+        qa(0, 0)
+        sort_h(0)
+
+        emission(0, 0)
+        sort_h(1)
+        al(nc.vector, 1, 0)
+        sort_h(2)
+        qa(1, 0)
+        emission(1, 0)
+        ei(0, 0)
+        sort_h(3)
+        qe(0, 0)
+        emission(2, 0)
+        al(nc.vector, 2, 0)
+        ei(1, 0)
+        nc.vector.tensor_copy(out=rows[TS_ROW : TS_ROW + R_TILES, 0, :], in_=rows_bf[TS_ROW : TS_ROW + R_TILES, 0:P])
+        qa(2, 0)
+        qe(1, 0)
+        emission(3, 0)
+        al(nc.vector, 3, 0)
+        ei(2, 0)
+        qa(3, 0)
+        qe(2, 0)
+        ts_bank = psum.tile([P, 4, P], F32, name="t_bank", tag="t_bank", bufs=2)
+        nc.tensor.transpose(ts_bank[:, 0, :], rows[:, 0, :], ident[:])
+        nc.vector.tensor_copy(out=ts_col[:], in_=ts_bank[:, 0, TS_ROW : TS_ROW + R_TILES])
+        for a in range(J_PASSES):
+            emission(a, 1)
+        ei(3, 0)
+        ei(0, 1)
+        qe(3, 0)
+        ei(1, 1)
+        qe(0, 1)
+        qe(1, 1)
+
+        V, S = nc.vector, nc.scalar
+        vector_extra = {
+            0: [lambda: ei(2, 1), lambda: ei(3, 1), lambda: qe(2, 1), lambda: qe(3, 1)],
+            1: [lambda: qa(0, 1), lambda: qa(1, 1)],
+            2: [lambda: qa(2, 1), lambda: qa(3, 1)],
+            3: [lambda: al(V, 3, 2), lambda: qa(0, 2)],
+            4: [lambda: qa(3, 2), lambda: qa(1, 2)],
+            5: [lambda: qa(2, 2)],
+        }
+        scalar_extra = {
+            0: [lambda: al(S, 0, 1), lambda: al(S, 1, 1)],
+            1: [lambda: al(S, 2, 1), lambda: al(S, 3, 1)],
+            2: [lambda: al(S, 0, 2)],
+            3: [lambda: al(S, 1, 2)],
+            4: [lambda: al(S, 2, 2)],
+        }
+        pairs = M_CHUNKS * R_TILES // 2
+        LR, LT, LL, LP = 1, 2, 2, 3
+        for k in range(pairs + LP):
+            if k < pairs:
+                product(2 * k)
+                scale_d(2 * k)
+                product(2 * k + 1)
+                scale_d(2 * k + 1)
+            if 0 <= k - LT < pairs:
+                turn(k - LT)
+            for step in scalar_extra.get(k, []):
+                step()
+            if 0 <= k - LR < pairs:
+                round_y(2 * (k - LR), S)
+                round_y(2 * (k - LR) + 1, V if k - LR == pairs - 1 else S)
+            if 0 <= k - LL < pairs:
+                leave(k - LL)
+            for step in vector_extra.get(k, []):
+                step()
+            if 0 <= k - LP < pairs:
+                planes(k - LP)
+            if k < pairs:
+                finish(2 * k)
+                finish(2 * k + 1)

@@ -24,6 +24,9 @@ M_CHUNKS = M // PASS
 R_TILES = R // P
 R_CHUNKS = ((0, 512), (512, 256))
 TS_ROW = 32
+BASE_ROW = 64
+G_COLS = 352
+USE_G = False
 
 
 def tile_haplotype_emission_alleles_k5_kernel(
@@ -44,9 +47,10 @@ def tile_haplotype_emission_alleles_k5_kernel(
         rows = kept("rows", [P, 4, P], F32)
         ln_w = kept("ln_w", [P, 4, J_PASSES], F32)
         ts_col = kept("ts_col", [P, R_TILES], F32)
-        warm = kept("warm", [P, 2], F32)
+        one = kept("one", [P, 1], F32)
+        vec_rows = kept("vec_rows", [P, P], F32)
         gain_bc = kept("gain_bc", [P, M], BF16)
-        base_bc = kept("base_bc", [P, M], BF16)
+        base_col = kept("base_col", [P, M // P], F32)
         c_codes = [kept("c_codes%d" % c, [P, K_PASSES, 2 * R_CHUNKS[c][1]], U8) for c in range(2)]
         c_plane = kept("c_plane", [P, K_PASSES, R], U8)
         h_plane_raw = kept("h_plane_raw", [P, K_PASSES, J], U8)
@@ -57,18 +61,22 @@ def tile_haplotype_emission_alleles_k5_kernel(
         a_rest = [kept("a_rest%d" % a, [P, 4, M - PASS], BF16) for a in range(J_PASSES)]
         a_codes = {(a, g): kept("a_codes%d_%d" % (a, g), [P, PASS], U32) for a in range(J_PASSES) for g in range(M_CHUNKS)}
         a_plane = {(a, g): kept("a_plane%d_%d" % (a, g), [P, PASS], U8) for a in range(J_PASSES) for g in range(M_CHUNKS)}
-        e_rows = {(a, c): kept("e_rows%d_%d" % (a, c), [P, 4, R_CHUNKS[c][1]], BF16) for a in range(J_PASSES) for c in range(2)}
-        e_codes = {(a, c): kept("e_codes%d_%d" % (a, c), [P, R_CHUNKS[c][1]], U32) for a in range(J_PASSES) for c in range(2)}
-        e_plane = {(a, c): kept("e_plane%d_%d" % (a, c), [P, R_CHUNKS[c][1]], U8) for a in range(J_PASSES) for c in range(2)}
+        e_keys = [(a, 0) for a in range(J_PASSES)] + [(0, 1), (2, 1)]
+        e_rows = {k: kept("e_rows%d_%d" % k, [P, 4, PASS], BF16) for k in e_keys}
+        e_codes = {k: kept("e_codes%d_%d" % k, [P, PASS], U32) for k in e_keys}
+        e_plane = {k: kept("e_plane%d_%d" % k, [P, PASS], U8) for k in e_keys}
+
+        def e_place(a, c):
+            return ((a, 0), 0) if c == 0 else ((a - a % 2, 1), (a % 2) * R_CHUNKS[1][1])
+
+        y_codes = [kept("y_codes%d" % g, [P, R], U32) for g in range(M_CHUNKS)]
         y_plane = [kept("y_plane%d" % g, [P, R], U8) for g in range(M_CHUNKS)]
 
-        nc.vector.memset(warm[:], 1.0)
+        nc.vector.memset(one[:], 1.0)
         nc.vector.memset(h_plane_raw[:].rearrange("p g n -> p (g n)").bitcast(I32), 0)
-        nc.vector.memset(rows[:], 0.0)
         nc.vector.memset(ident[:], 0.0)
         nc.vector.memset(c_plane[:].rearrange("p g n -> p (g n)").bitcast(I32), 0)
-        nc.scalar.activation(out=warm[:, 1:2], in_=warm[:, 0:1], func=ACT.Ln)
-        make_identity(nc, ident[:], nomemset=True)
+        nc.scalar.activation(out=rows[:].rearrange("p t n -> p (t n)"), in_=one[:].to_broadcast([P, PASS]), func=ACT.Ln)
 
         def load_plane(queue, plane, scales, quadrants):
             for q in quadrants:
@@ -95,6 +103,7 @@ def tile_haplotype_emission_alleles_k5_kernel(
                 in_=c_words[:, :, 2 * r0 : 2 * (r0 + width)].rearrange("g p n -> p g n").bitcast(I32),
             )
 
+        make_identity(nc, ident[:], nomemset=True)
         nc.sync.dma_start(out=rows_bf[0:J_PASSES, :], in_=hap_weight.rearrange("(a n) -> a n", n=PASS))
         load_alleles(a_first[0], 0, slice(0, PASS))
         load_plane(nc.sync, h_plane_raw, h_scales, (0,))
@@ -106,41 +115,42 @@ def tile_haplotype_emission_alleles_k5_kernel(
         load_alleles(a_first[1], 1, slice(0, PASS))
         load_h(2)
         load_h(3)
-        nc.sync.dma_start(out=rows_bf[TS_ROW : TS_ROW + R_TILES, 0:P], in_=target_scale.rearrange("(a n) -> a n", n=P))
         load_alleles(a_first[2], 2, slice(0, PASS))
+        nc.sync.dma_start(out=rows_bf[TS_ROW : TS_ROW + R_TILES, 0:P], in_=target_scale.rearrange("(a n) -> a n", n=P))
+        nc.sync.dma_start(out=rows_bf[BASE_ROW : BASE_ROW + M // P, 0:P], in_=base.rearrange("(a n) -> a n", n=P))
         load_alleles(a_first[3], 3, slice(0, PASS))
         load_c(1)
         nc.sync.dma_start(out=gain_bc[:], in_=marker_gain.partition_broadcast(P))
-        nc.sync.dma_start(out=base_bc[:], in_=base.partition_broadcast(P))
         for a in range(J_PASSES):
             load_alleles(a_rest[a], a, slice(PASS, M))
 
         grouped = {}
 
-        def interleave(engine, key, src):
-            width = src.shape[2]
-            tag = "by_scalar" if engine is nc.scalar else "by_vector"
-            dst = work.tile([P, width, 4], BF16, name=tag, tag=tag, bufs=4, align_bytes=64)
-            grouped[key] = dst
-            o = dst[:].rearrange("p (c i) t -> p c t i", i=4)
-            s = src.rearrange("p t (c i) -> p c t i", i=4)
+        def interleave(engine, key, src, tag=None, cols=slice(0, PASS)):
+            if key not in grouped:
+                tag = tag or ("by_scalar" if engine is nc.scalar else "by_vector")
+                grouped[key] = work.tile([P, PASS, 4], BF16, name=tag, tag=tag, bufs=1 if tag == "by_gpsimd" else 3, align_bytes=64)
+            o = grouped[key][:, cols, :].rearrange("p (c i) t -> p c t i", i=4)
+            s = src[:, :, cols].rearrange("p t (c i) -> p c t i", i=4)
             if engine is nc.scalar:
                 nc.scalar.copy(out=o, in_=s)
+            elif engine is nc.gpsimd:
+                nc.gpsimd.tensor_scalar(out=grouped[key][:, cols, :], in0=src[:, :, cols].rearrange("p t c -> p c t"), scalar1=1.0, scalar2=-0.0, op0=ALU.mult, op1=ALU.add)
             else:
                 nc.vector.tensor_copy(out=o, in_=s)
 
         def quantise(key, codes, plane):
             nc.vector.quantize_mx(out=codes.bitcast(FP8X4), scales=plane, in_=grouped[key][:].rearrange("p c t -> p (c t)"))
 
-        def al(engine, a, g):
+        def al(engine, a, g, tag=None, cols=slice(0, PASS)):
             src = a_first[a][:] if g == 0 else a_rest[a][:, :, PASS * (g - 1) : PASS * g]
-            interleave(engine, ("a", a, g), src)
+            interleave(engine, ("a", a, g), src, tag, cols)
 
         def qa(a, g):
             quantise(("a", a, g), a_codes[a, g][:], a_plane[a, g][:])
 
-        def ei(a, c):
-            interleave(nc.vector, ("e", a, c), e_rows[a, c][:])
+        def ei(a, c, engine=nc.vector, tag=None):
+            interleave(engine, ("e", a, c), e_rows[a, c][:], tag)
 
         def qe(a, c):
             quantise(("e", a, c), e_codes[a, c][:], e_plane[a, c][:])
@@ -157,8 +167,9 @@ def tile_haplotype_emission_alleles_k5_kernel(
 
         def emission(a, c):
             r0, width = R_CHUNKS[c]
+            key, off = e_place(a, c)
             for t in range(4):
-                bank = psum.tile([P, PASS], F32, name="s_bank", tag="s_bank", bufs=3)
+                bank = psum.tile([P, PASS], F32, name="s_bank", tag="mx_bank", bufs=5)
                 for g in range(K_PASSES):
                     nc.tensor.matmul_mx(
                         out=bank[:, 0:width],
@@ -169,20 +180,21 @@ def tile_haplotype_emission_alleles_k5_kernel(
                         start=(g == 0),
                         stop=(g == K_PASSES - 1),
                     )
-                nc.scalar.activation(out=e_rows[a, c][:, t, :], in_=bank[:, 0:width], func=ACT.Exp, bias=ln_w[:, t, a : a + 1])
+                nc.scalar.activation(out=e_rows[key][:, t, off : off + width], in_=bank[:, 0:width], func=ACT.Exp, bias=ln_w[:, t, a : a + 1])
 
-        d_of, z_of, y_of, yb_of, tb_of, yg_of = {}, {}, {}, {}, {}, {}
+        base_bank, d_of, z_of, y_of, yb_of, tb_of, yg_of = {}, {}, {}, {}, {}, {}, {}
 
         def product(n):
             g, rt = divmod(n, R_TILES)
             c = 0 if rt < 4 else 1
-            cols = slice(P * rt - R_CHUNKS[c][0], P * (rt + 1) - R_CHUNKS[c][0])
-            bank = psum.tile([P, PASS], F32, name="d_bank", tag="d_bank", bufs=3)
+            bank = psum.tile([P, PASS], F32, name="d_bank", tag="mx_bank", bufs=5)
             for a in range(J_PASSES):
+                key, off = e_place(a, c)
+                cols = slice(off + P * rt - R_CHUNKS[c][0], off + P * (rt + 1) - R_CHUNKS[c][0])
                 nc.tensor.matmul_mx(
                     out=bank[:],
-                    lhsT=e_codes[a, c][:, cols].bitcast(FP8X4),
-                    lhsT_scale=e_plane[a, c][:, cols],
+                    lhsT=e_codes[key][:, cols].bitcast(FP8X4),
+                    lhsT_scale=e_plane[key][:, cols],
                     rhs=a_codes[a, g][:].bitcast(FP8X4),
                     rhs_scale=a_plane[a, g][:],
                     start=(a == 0),
@@ -192,62 +204,73 @@ def tile_haplotype_emission_alleles_k5_kernel(
 
         def scale_d(n):
             g, rt = divmod(n, R_TILES)
-            bank = d_of[n]
-            z = work.tile([P, PASS], F32, name="z", tag="z", bufs=3)
-            z_of[n] = z
+            if n % 2 == 0:
+                z_of[n // 2] = work.tile([P, 2, PASS], F32, name="z", tag="z", bufs=2)
             nc.vector.scalar_tensor_tensor(
-                out=z[:], in0=bank[:], scalar=ts_col[:, rt : rt + 1], in1=gain_bc[:, PASS * g : PASS * (g + 1)],
+                out=z_of[n // 2][:, n % 2, :], in0=d_of[n][:], scalar=ts_col[:, rt : rt + 1], in1=gain_bc[:, PASS * g : PASS * (g + 1)],
                 op0=ALU.mult, op1=ALU.mult,
             )
 
-        def finish(n):
-            g, rt = divmod(n, R_TILES)
-            y = work.tile([P, PASS], F32, name="y", tag="y", bufs=8)
-            y_of[n] = y
-            nc.vector.tensor_tensor(out=y[:], in0=z_of[n][:], in1=base_bc[:, PASS * g : PASS * (g + 1)], op=ALU.add)
-            nc.sync.dma_start(out=out_0[P * rt : P * (rt + 1), PASS * g : PASS * (g + 1)], in_=y[:])
+        def spread_base(g):
+            bank = psum.tile([P, PASS], F32, name="b_bank", tag="b_bank", bufs=1)
+            base_bank[g] = bank
+            for c in range(4):
+                nc.tensor.transpose(bank[:, P * c : P * (c + 1)], base_col[:, 4 * g + c : 4 * g + c + 1].to_broadcast([P, P]), ident[:])
 
-        def round_y(n, engine):
-            yb = work.tile([P, 2, P, 2], BF16, name="yb", tag="yb", bufs=4, align_bytes=64)
-            yb_of[n] = yb
-            src = y_of[n][:].rearrange("r (p u e) -> r u p e", u=2, e=2)
+        def finish(pair, h0, h1):
+            g, k = divmod(pair, R_TILES // 2)
+            if h0 == 0:
+                y_of[pair] = work.tile([P, 2, PASS], F32, name="y", tag="y", bufs=4)
+            y = y_of[pair][:, h0:h1, :]
+            nc.vector.tensor_tensor(
+                out=y, in0=z_of[pair][:, h0:h1, :], in1=base_bank[g][:].unsqueeze(1).to_broadcast([P, h1 - h0, PASS]), op=ALU.add
+            )
+            rows_out = out_0[P * (2 * k + h0) : P * (2 * k + h1), PASS * g : PASS * (g + 1)]
+            nc.sync.dma_start(out=rows_out.rearrange("(h r) m -> r h m", r=P), in_=y)
+
+        def round_y(pair, h0, h1, engine):
+            if h0 == 0:
+                yb_of[pair] = work.tile([P, 2, 2, P, 2], BF16, name="yb", tag="yb", bufs=2, align_bytes=64)
+            src = y_of[pair][:, h0:h1, :].rearrange("r h (p u e) -> r h u p e", u=2, e=2)
             if engine is nc.scalar:
-                nc.scalar.copy(out=yb[:], in_=src)
+                nc.scalar.copy(out=yb_of[pair][:, h0:h1], in_=src)
             else:
-                nc.vector.tensor_copy(out=yb[:], in_=src)
+                nc.vector.tensor_copy(out=yb_of[pair][:, h0:h1], in_=src)
 
-        def turn(pair):
+        def turn(pair, h0, h1):
             bank = psum.tile([P, 2, 2, P], F32, name="t_bank", tag="t_bank", bufs=2)
-            tb_of[pair] = bank
-            for h in range(2):
-                words = yb_of[2 * pair + h][:].rearrange("r u p e -> r (u p e)").bitcast(F32)
+            tb_of[pair, h0] = bank
+            for h in range(h0, h1):
+                words = yb_of[pair][:, h].rearrange("r u p e -> r (u p e)").bitcast(F32)
                 for u in range(2):
-                    nc.tensor.transpose(bank[:, h, u, :], words[:, P * u : P * (u + 1)], ident[:])
+                    nc.tensor.transpose(bank[:, h - h0, u, :], words[:, P * u : P * (u + 1)], ident[:])
 
-        def leave(pair):
-            yg = work.tile([P, 2 * P * 4], BF16, name="yg", tag="yg", bufs=3, align_bytes=64)
-            yg_of[pair] = yg
+        def leave(pair, h0, h1):
+            yg = work.tile([P, (h1 - h0) * P * 4], BF16, name="yg", tag="yg", bufs=4, align_bytes=64)
+            yg_of[pair, h0] = yg
             nc.scalar.copy(
-                out=yg[:].bitcast(F32).rearrange("p (h r u) -> p h r u", h=2, u=2),
-                in_=tb_of[pair][:].rearrange("p h u r -> p h r u"),
+                out=yg[:].bitcast(F32).rearrange("p (h r u) -> p h r u", r=P, u=2),
+                in_=tb_of[pair, h0][:, 0 : h1 - h0].rearrange("p h u r -> p h r u"),
             )
 
-        def planes(pair):
+        def planes(pair, h0, h1):
             g, k = divmod(pair, R_TILES // 2)
-            cols = slice(2 * P * k, 2 * P * (k + 1))
-            codes = work.tile([P, 2 * P], U32, name="y_codes", tag="y_codes", bufs=3, align_bytes=64)
-            nc.vector.quantize_mx(out=codes[:].bitcast(FP8X4), scales=y_plane[g][:, cols], in_=yg_of[pair][:])
-            nc.sync.dma_start(out=out_1[g, :, cols, :].rearrange("p m t -> p (m t)").bitcast(I32), in_=codes[:].bitcast(I32))
-            if k == R_TILES // 2 - 1:
+            cols = slice(P * (2 * k + h0), P * (2 * k + h1))
+            nc.vector.quantize_mx(out=y_codes[g][:, cols].bitcast(FP8X4), scales=y_plane[g][:, cols], in_=yg_of[pair, h0][:])
+            if cols.stop == R or (pair, h1) == (last, 1):
+                done = slice(R - P if (pair, h0) == (last, 1) else 0, cols.stop)
+                nc.sync.dma_start(out=out_1[g, :, done, :].rearrange("p m t -> p (m t)").bitcast(I32), in_=y_codes[g][:, done].bitcast(I32))
+            if cols.stop == R:
+                queue = nc.scalar if g == M_CHUNKS - 1 else nc.sync
                 for q in range(4):
-                    nc.sync.dma_start(out=out_2[g, 4 * q : 4 * q + 4, :].bitcast(I32), in_=y_plane[g][32 * q : 32 * q + 4, :].bitcast(I32))
+                    queue.dma_start(out=out_2[g, 4 * q : 4 * q + 4, :].bitcast(I32), in_=y_plane[g][32 * q : 32 * q + 4, :].bitcast(I32))
 
         nc.scalar.activation(
             out=rows[0:J_PASSES, :, :].rearrange("a t (s i) -> a t s i", i=4),
             in_=rows_bf[0:J_PASSES, :].rearrange("a (s t i) -> a t s i", t=4, i=4),
             func=ACT.Ln,
         )
-        nc.scalar.activation(out=warm[:, 1:2], in_=warm[:, 0:1], func=ACT.Exp)
+        nc.scalar.activation(out=vec_rows[:], in_=one[:].to_broadcast([P, P]), func=ACT.Exp)
         al(nc.vector, 0, 0)
         col_bank = psum.tile([P, 4, P], F32, name="t_bank", tag="t_bank", bufs=2)
         for t in range(4):
@@ -268,63 +291,88 @@ def tile_haplotype_emission_alleles_k5_kernel(
         emission(2, 0)
         al(nc.vector, 2, 0)
         ei(1, 0)
-        nc.vector.tensor_copy(out=rows[TS_ROW : TS_ROW + R_TILES, 0, :], in_=rows_bf[TS_ROW : TS_ROW + R_TILES, 0:P])
+        nc.vector.tensor_copy(out=vec_rows[TS_ROW : TS_ROW + R_TILES, :], in_=rows_bf[TS_ROW : TS_ROW + R_TILES, 0:P])
+        nc.vector.tensor_copy(out=vec_rows[BASE_ROW : BASE_ROW + M // P, :], in_=rows_bf[BASE_ROW : BASE_ROW + M // P, 0:P])
         qa(2, 0)
         qe(1, 0)
         emission(3, 0)
-        al(nc.vector, 3, 0)
+        V, S, G = nc.vector, nc.scalar, nc.gpsimd
+        mine, rest = slice(0, G_COLS), slice(G_COLS, PASS)
+        ts_bank = psum.tile([P, 4, P], F32, name="t_bank", tag="t_bank", bufs=2)
+        nc.tensor.transpose(ts_bank[:, 0, :], vec_rows[:], ident[:])
+        nc.vector.tensor_copy(out=ts_col[:], in_=ts_bank[:, 0, TS_ROW : TS_ROW + R_TILES])
+        nc.vector.tensor_copy(out=base_col[:], in_=ts_bank[:, 0, BASE_ROW : BASE_ROW + M // P])
+        al(V, 3, 0)
         ei(2, 0)
         qa(3, 0)
-        qe(2, 0)
-        ts_bank = psum.tile([P, 4, P], F32, name="t_bank", tag="t_bank", bufs=2)
-        nc.tensor.transpose(ts_bank[:, 0, :], rows[:, 0, :], ident[:])
-        nc.vector.tensor_copy(out=ts_col[:], in_=ts_bank[:, 0, TS_ROW : TS_ROW + R_TILES])
-        for a in range(J_PASSES):
-            emission(a, 1)
+        emission(0, 1)
+        spread_base(0)
+        emission(1, 1)
         ei(3, 0)
-        ei(0, 1)
+        qe(2, 0)
+        emission(2, 1)
+        emission(3, 1)
         qe(3, 0)
-        ei(1, 1)
-        qe(0, 1)
-        qe(1, 1)
-
-        V, S = nc.vector, nc.scalar
+        ei(0, 1, V, "by_gpsimd")
+        between = {0: [lambda: qe(0, 1), lambda: al(G, 2, 1, "by_gpsimd", mine)]}
+        after = {}
         vector_extra = {
-            0: [lambda: ei(2, 1), lambda: ei(3, 1), lambda: qe(2, 1), lambda: qe(3, 1)],
-            1: [lambda: qa(0, 1), lambda: qa(1, 1)],
-            2: [lambda: qa(2, 1), lambda: qa(3, 1)],
-            3: [lambda: al(V, 3, 2), lambda: qa(0, 2)],
-            4: [lambda: qa(3, 2), lambda: qa(1, 2)],
-            5: [lambda: qa(2, 2)],
+            1: [lambda: qe(2, 1), lambda: qa(0, 1), lambda: qa(2, 1), lambda: al(G, 3, 1, "by_gpsimd", mine)],
+            2: [lambda: qa(1, 1), lambda: qa(3, 1), lambda: al(G, 1, 2, "by_gpsimd", mine)],
+            3: [lambda: qa(1, 2), lambda: al(G, 2, 2, "by_gpsimd", mine)],
+            4: [lambda: qa(0, 2), lambda: qa(2, 2), lambda: al(G, 3, 2, "by_gpsimd", mine)],
+            5: [lambda: qa(3, 2)],
         }
         scalar_extra = {
-            0: [lambda: al(S, 0, 1), lambda: al(S, 1, 1)],
-            1: [lambda: al(S, 2, 1), lambda: al(S, 3, 1)],
-            2: [lambda: al(S, 0, 2)],
-            3: [lambda: al(S, 1, 2)],
-            4: [lambda: al(S, 2, 2)],
+            0: [lambda: ei(2, 1, S), lambda: al(S, 0, 1)],
+            1: [lambda: al(S, 2, 1, None, rest), lambda: al(S, 1, 1)],
+            2: [lambda: al(S, 3, 1, None, rest)],
+            3: [lambda: al(S, 1, 2, None, rest), lambda: al(S, 0, 2)],
+            4: [lambda: al(S, 2, 2, None, rest)],
+            5: [lambda: al(S, 3, 2, None, rest)],
         }
         pairs = M_CHUNKS * R_TILES // 2
+        last = pairs - 1
         LR, LT, LL, LP = 1, 2, 2, 3
-        for k in range(pairs + LP):
+        for k in range(pairs):
             if k < pairs:
                 product(2 * k)
                 scale_d(2 * k)
+                for step in between.get(k, []):
+                    step()
                 product(2 * k + 1)
-                scale_d(2 * k + 1)
+                if k % 3 == 0 and k > 0:
+                    spread_base(k // 3)
+                if k < last:
+                    scale_d(2 * k + 1)
+            for step in after.get(k, []):
+                step()
             if 0 <= k - LT < pairs:
-                turn(k - LT)
+                turn(k - LT, 0, 2)
             for step in scalar_extra.get(k, []):
                 step()
-            if 0 <= k - LR < pairs:
-                round_y(2 * (k - LR), S)
-                round_y(2 * (k - LR) + 1, V if k - LR == pairs - 1 else S)
+            if 0 <= k - LR < last:
+                round_y(k - LR, 0, 2, S)
             if 0 <= k - LL < pairs:
-                leave(k - LL)
+                leave(k - LL, 0, 2)
+            if 0 <= k - LP < pairs:
+                planes(k - LP, 0, 2)
             for step in vector_extra.get(k, []):
                 step()
-            if 0 <= k - LP < pairs:
-                planes(k - LP)
-            if k < pairs:
-                finish(2 * k)
-                finish(2 * k + 1)
+            if k < last:
+                finish(k, 0, 2)
+        finish(last, 0, 1)
+        round_y(last, 0, 1, S)
+        scale_d(2 * last + 1)
+        finish(last, 1, 2)
+        turn(last - 1, 0, 2)
+        leave(last - 1, 0, 2)
+        turn(last, 0, 1)
+        leave(last, 0, 1)
+        round_y(last, 1, 2, V)
+        planes(last - 2, 0, 2)
+        planes(last - 1, 0, 2)
+        turn(last, 1, 2)
+        leave(last, 1, 2)
+        planes(last, 0, 1)
+        planes(last, 1, 2)

@@ -23,8 +23,9 @@ J_PASSES = J // PASS
 M_CHUNKS = M // PASS
 R_TILES = R // P
 R_CHUNKS = ((0, 512), (512, 256))
-TS_ROW = 32
-BASE_ROW = 64
+TS_ROW = 64
+BASE_ROW = TS_ROW + R_TILES
+VEC_END = BASE_ROW + M // P
 G_COLS = 352
 USE_G = False
 
@@ -46,19 +47,17 @@ def tile_haplotype_emission_alleles_k5_kernel(
         rows_bf = kept("rows_bf", [P, PASS], BF16)
         rows = kept("rows", [P, 4, P], F32)
         ln_w = kept("ln_w", [P, 4, J_PASSES], F32)
-        ts_col = kept("ts_col", [P, R_TILES], F32)
+        vec_cols = kept("vec_cols", [P, VEC_END - TS_ROW], F32)
         one = kept("one", [P, 1], F32)
         vec_rows = kept("vec_rows", [P, P], F32)
-        gain_bc = kept("gain_bc", [P, M], BF16)
-        base_col = kept("base_col", [P, M // P], F32)
+        gain_bc = [kept("gain_bc%d" % g, [P, PASS], BF16) for g in range(M_CHUNKS)]
         c_codes = [kept("c_codes%d" % c, [P, K_PASSES, 2 * R_CHUNKS[c][1]], U8) for c in range(2)]
         c_plane = kept("c_plane", [P, K_PASSES, R], U8)
         h_plane_raw = kept("h_plane_raw", [P, K_PASSES, J], U8)
         h_raw = [kept("h_raw%d" % a, [P, K_PASSES, 2 * PASS], U8) for a in range(J_PASSES)]
         h_codes = [kept("h_codes%d" % a, [P, K_PASSES, 4, 2 * P], U8) for a in range(J_PASSES)]
         h_plane = [kept("h_plane%d" % a, [P, K_PASSES, 4, P], U8) for a in range(J_PASSES)]
-        a_first = [kept("a_first%d" % a, [P, 4, PASS], BF16) for a in range(J_PASSES)]
-        a_rest = [kept("a_rest%d" % a, [P, 4, M - PASS], BF16) for a in range(J_PASSES)]
+        a_rows = {(a, g): kept("a_rows%d_%d" % (a, g), [P, 4, PASS], BF16) for a in range(J_PASSES) for g in range(M_CHUNKS)}
         a_codes = {(a, g): kept("a_codes%d_%d" % (a, g), [P, PASS], U32) for a in range(J_PASSES) for g in range(M_CHUNKS)}
         a_plane = {(a, g): kept("a_plane%d_%d" % (a, g), [P, PASS], U8) for a in range(J_PASSES) for g in range(M_CHUNKS)}
         e_keys = [(a, 0) for a in range(J_PASSES)] + [(0, 1), (2, 1)]
@@ -85,8 +84,9 @@ def tile_haplotype_emission_alleles_k5_kernel(
                     in_=scales[:, 4 * q : 4 * q + 4, :].rearrange("g r n -> r g n").bitcast(I32),
                 )
 
-        def load_alleles(dst, a, cols):
-            src = alleles[PASS * a : PASS * (a + 1), cols].rearrange("(s t i) m -> i s t m", t=4, i=4)
+        def load_alleles(a, g):
+            dst = a_rows[a, g]
+            src = alleles[PASS * a : PASS * (a + 1), PASS * g : PASS * (g + 1)].rearrange("(s t i) m -> i s t m", t=4, i=4)
             for i in range(4):
                 nc.sync.dma_start(out=dst[i:P:4, :, :], in_=src[i])
 
@@ -105,24 +105,26 @@ def tile_haplotype_emission_alleles_k5_kernel(
 
         make_identity(nc, ident[:], nomemset=True)
         nc.sync.dma_start(out=rows_bf[0:J_PASSES, :], in_=hap_weight.rearrange("(a n) -> a n", n=PASS))
-        load_alleles(a_first[0], 0, slice(0, PASS))
+        load_alleles(0, 0)
         load_plane(nc.sync, h_plane_raw, h_scales, (0,))
         load_h(0)
         load_c(0)
         load_plane(nc.sync, h_plane_raw, h_scales, (1, 2, 3))
         load_plane(nc.sync, c_plane, c_scales, (0, 1, 2, 3))
         load_h(1)
-        load_alleles(a_first[1], 1, slice(0, PASS))
+        load_alleles(1, 0)
         load_h(2)
         load_h(3)
-        load_alleles(a_first[2], 2, slice(0, PASS))
+        load_alleles(2, 0)
         nc.sync.dma_start(out=rows_bf[TS_ROW : TS_ROW + R_TILES, 0:P], in_=target_scale.rearrange("(a n) -> a n", n=P))
         nc.sync.dma_start(out=rows_bf[BASE_ROW : BASE_ROW + M // P, 0:P], in_=base.rearrange("(a n) -> a n", n=P))
-        load_alleles(a_first[3], 3, slice(0, PASS))
+        load_alleles(3, 0)
         load_c(1)
-        nc.sync.dma_start(out=gain_bc[:], in_=marker_gain.partition_broadcast(P))
-        for a in range(J_PASSES):
-            load_alleles(a_rest[a], a, slice(PASS, M))
+        nc.sync.dma_start(out=gain_bc[0][:], in_=marker_gain[0:PASS].partition_broadcast(P))
+        for g in range(1, M_CHUNKS):
+            for a in range(J_PASSES):
+                load_alleles(a, g)
+            nc.sync.dma_start(out=gain_bc[g][:], in_=marker_gain[PASS * g : PASS * (g + 1)].partition_broadcast(P))
 
         grouped = {}
 
@@ -143,7 +145,7 @@ def tile_haplotype_emission_alleles_k5_kernel(
             nc.vector.quantize_mx(out=codes.bitcast(FP8X4), scales=plane, in_=grouped[key][:].rearrange("p c t -> p (c t)"))
 
         def al(engine, a, g, tag=None, cols=slice(0, PASS)):
-            src = a_first[a][:] if g == 0 else a_rest[a][:, :, PASS * (g - 1) : PASS * g]
+            src = a_rows[a, g][:]
             interleave(engine, ("a", a, g), src, tag, cols)
 
         def qa(a, g):
@@ -169,7 +171,7 @@ def tile_haplotype_emission_alleles_k5_kernel(
             r0, width = R_CHUNKS[c]
             key, off = e_place(a, c)
             for t in range(4):
-                bank = psum.tile([P, PASS], F32, name="s_bank", tag="mx_bank", bufs=5)
+                bank = psum.tile([P, PASS], F32, name="s_bank", tag="mx_bank", bufs=4)
                 for g in range(K_PASSES):
                     nc.tensor.matmul_mx(
                         out=bank[:, 0:width],
@@ -184,15 +186,16 @@ def tile_haplotype_emission_alleles_k5_kernel(
 
         base_bank, d_of, z_of, y_of, yb_of, tb_of, yg_of = {}, {}, {}, {}, {}, {}, {}
 
-        def product(n):
+        def product(n, passes=range(J_PASSES)):
             g, rt = divmod(n, R_TILES)
             c = 0 if rt < 4 else 1
-            bank = psum.tile([P, PASS], F32, name="d_bank", tag="mx_bank", bufs=5)
-            for a in range(J_PASSES):
+            if n not in d_of:
+                d_of[n] = psum.tile([P, PASS], F32, name="d_bank", tag="mx_bank", bufs=4)
+            for a in passes:
                 key, off = e_place(a, c)
                 cols = slice(off + P * rt - R_CHUNKS[c][0], off + P * (rt + 1) - R_CHUNKS[c][0])
                 nc.tensor.matmul_mx(
-                    out=bank[:],
+                    out=d_of[n][:],
                     lhsT=e_codes[key][:, cols].bitcast(FP8X4),
                     lhsT_scale=e_plane[key][:, cols],
                     rhs=a_codes[a, g][:].bitcast(FP8X4),
@@ -200,22 +203,21 @@ def tile_haplotype_emission_alleles_k5_kernel(
                     start=(a == 0),
                     stop=(a == J_PASSES - 1),
                 )
-            d_of[n] = bank
 
         def scale_d(n):
             g, rt = divmod(n, R_TILES)
             if n % 2 == 0:
                 z_of[n // 2] = work.tile([P, 2, PASS], F32, name="z", tag="z", bufs=2)
             nc.vector.scalar_tensor_tensor(
-                out=z_of[n // 2][:, n % 2, :], in0=d_of[n][:], scalar=ts_col[:, rt : rt + 1], in1=gain_bc[:, PASS * g : PASS * (g + 1)],
+                out=z_of[n // 2][:, n % 2, :], in0=d_of[n][:], scalar=vec_cols[:, rt : rt + 1], in1=gain_bc[g][:],
                 op0=ALU.mult, op1=ALU.mult,
             )
 
         def spread_base(g):
-            bank = psum.tile([P, PASS], F32, name="b_bank", tag="b_bank", bufs=1)
+            bank = psum.tile([P, PASS], F32, name="b_bank", tag="b_bank", bufs=2)
             base_bank[g] = bank
             for c in range(4):
-                nc.tensor.transpose(bank[:, P * c : P * (c + 1)], base_col[:, 4 * g + c : 4 * g + c + 1].to_broadcast([P, P]), ident[:])
+                nc.tensor.transpose(bank[:, P * c : P * (c + 1)], vec_cols[:, R_TILES + 4 * g + c : R_TILES + 4 * g + c + 1].to_broadcast([P, P]), ident[:])
 
         def finish(pair, h0, h1):
             g, k = divmod(pair, R_TILES // 2)
@@ -291,8 +293,7 @@ def tile_haplotype_emission_alleles_k5_kernel(
         emission(2, 0)
         al(nc.vector, 2, 0)
         ei(1, 0)
-        nc.vector.tensor_copy(out=vec_rows[TS_ROW : TS_ROW + R_TILES, :], in_=rows_bf[TS_ROW : TS_ROW + R_TILES, 0:P])
-        nc.vector.tensor_copy(out=vec_rows[BASE_ROW : BASE_ROW + M // P, :], in_=rows_bf[BASE_ROW : BASE_ROW + M // P, 0:P])
+        nc.vector.tensor_copy(out=vec_rows[TS_ROW:VEC_END, :], in_=rows_bf[TS_ROW:VEC_END, 0:P])
         qa(2, 0)
         qe(1, 0)
         emission(3, 0)
@@ -300,8 +301,7 @@ def tile_haplotype_emission_alleles_k5_kernel(
         mine, rest = slice(0, G_COLS), slice(G_COLS, PASS)
         ts_bank = psum.tile([P, 4, P], F32, name="t_bank", tag="t_bank", bufs=2)
         nc.tensor.transpose(ts_bank[:, 0, :], vec_rows[:], ident[:])
-        nc.vector.tensor_copy(out=ts_col[:], in_=ts_bank[:, 0, TS_ROW : TS_ROW + R_TILES])
-        nc.vector.tensor_copy(out=base_col[:], in_=ts_bank[:, 0, BASE_ROW : BASE_ROW + M // P])
+        nc.vector.tensor_copy(out=vec_cols[:], in_=ts_bank[:, 0, TS_ROW:VEC_END])
         al(V, 3, 0)
         ei(2, 0)
         qa(3, 0)
@@ -314,20 +314,20 @@ def tile_haplotype_emission_alleles_k5_kernel(
         emission(3, 1)
         qe(3, 0)
         ei(0, 1, V, "by_gpsimd")
-        between = {0: [lambda: qe(0, 1), lambda: al(G, 2, 1, "by_gpsimd", mine)]}
+        between = {0: [lambda: qe(0, 1), lambda: al(G, 1, 1, "by_gpsimd", mine)]}
         after = {}
         vector_extra = {
-            1: [lambda: qe(2, 1), lambda: qa(0, 1), lambda: qa(2, 1), lambda: al(G, 3, 1, "by_gpsimd", mine)],
-            2: [lambda: qa(1, 1), lambda: qa(3, 1), lambda: al(G, 1, 2, "by_gpsimd", mine)],
-            3: [lambda: qa(1, 2), lambda: al(G, 2, 2, "by_gpsimd", mine)],
-            4: [lambda: qa(0, 2), lambda: qa(2, 2), lambda: al(G, 3, 2, "by_gpsimd", mine)],
+            1: [lambda: qe(2, 1), lambda: qa(0, 1), lambda: qa(1, 1), lambda: al(G, 3, 1, "by_gpsimd", mine)],
+            2: [lambda: qa(2, 1), lambda: qa(3, 1), lambda: al(G, 0, 2, "by_gpsimd", mine)],
+            3: [lambda: qa(0, 2), lambda: al(G, 2, 2, "by_gpsimd", mine)],
+            4: [lambda: qa(1, 2), lambda: qa(2, 2), lambda: al(G, 3, 2, "by_gpsimd", mine)],
             5: [lambda: qa(3, 2)],
         }
         scalar_extra = {
             0: [lambda: ei(2, 1, S), lambda: al(S, 0, 1)],
-            1: [lambda: al(S, 2, 1, None, rest), lambda: al(S, 1, 1)],
+            1: [lambda: al(S, 1, 1, None, rest)],
             2: [lambda: al(S, 3, 1, None, rest)],
-            3: [lambda: al(S, 1, 2, None, rest), lambda: al(S, 0, 2)],
+            3: [lambda: al(S, 0, 2, None, rest)],
             4: [lambda: al(S, 2, 2, None, rest)],
             5: [lambda: al(S, 3, 2, None, rest)],
         }
@@ -336,25 +336,32 @@ def tile_haplotype_emission_alleles_k5_kernel(
         LR, LT, LL, LP = 1, 2, 2, 3
         for k in range(pairs):
             if k < pairs:
-                product(2 * k)
+                if k < last:
+                    for a in range(J_PASSES):
+                        product(2 * k, [a])
+                        product(2 * k + 1, [a])
+                else:
+                    product(2 * k)
+                    product(2 * k + 1)
                 scale_d(2 * k)
                 for step in between.get(k, []):
                     step()
-                product(2 * k + 1)
-                if k % 3 == 0 and k > 0:
-                    spread_base(k // 3)
                 if k < last:
                     scale_d(2 * k + 1)
             for step in after.get(k, []):
                 step()
             if 0 <= k - LT < pairs:
                 turn(k - LT, 0, 2)
+            if k in (2, 4):
+                spread_base(k // 2)
             for step in scalar_extra.get(k, []):
                 step()
             if 0 <= k - LR < last:
                 round_y(k - LR, 0, 2, S)
             if 0 <= k - LL < pairs:
                 leave(k - LL, 0, 2)
+            if k in (1, 3):
+                al(S, 2 if k == 1 else 1, 1 if k == 1 else 2)
             if 0 <= k - LP < pairs:
                 planes(k - LP, 0, 2)
             for step in vector_extra.get(k, []):
@@ -364,12 +371,17 @@ def tile_haplotype_emission_alleles_k5_kernel(
         finish(last, 0, 1)
         round_y(last, 0, 1, S)
         scale_d(2 * last + 1)
+        nc.vector.tensor_tensor(
+            out=yb_of[last][:, 1],
+            in0=z_of[last][:, 1, :].rearrange("r (p u e) -> r u p e", u=2, e=2),
+            in1=base_bank[M_CHUNKS - 1][:].rearrange("r (p u e) -> r u p e", u=2, e=2),
+            op=ALU.add,
+        )
         finish(last, 1, 2)
         turn(last - 1, 0, 2)
         leave(last - 1, 0, 2)
         turn(last, 0, 1)
         leave(last, 0, 1)
-        round_y(last, 1, 2, V)
         planes(last - 2, 0, 2)
         planes(last - 1, 0, 2)
         turn(last, 1, 2)

@@ -17,23 +17,34 @@ ACT = mybir.ActivationFunctionType
 ALU = mybir.AluOpType
 
 P = 128
-PASS = 512
+SLOTS = 4
+PASS = P * SLOTS
 K_PASSES = K // PASS
 J_PASSES = J // PASS
 M_CHUNKS = M // PASS
 R_TILES = R // P
-R_CHUNKS = ((0, 512), (512, 256))
-TS_ROW = 64
-BASE_ROW = TS_ROW + R_TILES
-VEC_END = BASE_ROW + M // P
-G_COLS = 352
-USE_G = False
+PAIRS_PER_CHUNK = R_TILES // 2
+PAIRS = M_CHUNKS * PAIRS_PER_CHUNK
+LAST = PAIRS - 1
+LAST_CHUNK_START = PAIRS - PAIRS_PER_CHUNK
+
+WIDE, NARROW = 0, 1
+R_PARTS = ((0, 512), (512, 256))
+
+SCALE_ROW = 64
+BASE_ROW = SCALE_ROW + R_TILES
+END_ROW = BASE_ROW + M // P
+
+GPSIMD_PIECES = ((1, 1), (3, 1), (0, 2), (2, 2), (3, 2))
+GPSIMD_COLS = 320
+VECTOR_COLS = 256
 
 
 def tile_haplotype_emission_alleles_k5_kernel(
     tc, c_words, c_scales, h_words, h_scales, hap_weight, alleles, target_scale, marker_gain, base, out_0, out_1, out_2
 ):
     nc = tc.nc
+    vector, scalar, gpsimd = nc.vector, nc.scalar, nc.gpsimd
     with ExitStack() as ctx:
         keep = ctx.enter_context(tc.tile_pool(name="keep", bufs=1))
         work = ctx.enter_context(tc.tile_pool(name="work", bufs=1))
@@ -43,348 +54,398 @@ def tile_haplotype_emission_alleles_k5_kernel(
         def kept(name, shape, dtype):
             return keep.tile(shape, dtype, name=name, align_bytes=64)
 
+        def mx_bank():
+            return psum.tile([P, PASS], F32, name="mx_bank", tag="mx_bank", bufs=4)
+
+        def turn_bank():
+            return psum.tile([P, PASS], F32, name="turn_bank", tag="turn_bank", bufs=2)
+
+        pieces = [(a, g) for a in range(J_PASSES) for g in range(M_CHUNKS)]
         ident = kept("ident", [P, P], F32)
-        rows_bf = kept("rows_bf", [P, PASS], BF16)
-        rows = kept("rows", [P, 4, P], F32)
-        ln_w = kept("ln_w", [P, 4, J_PASSES], F32)
-        vec_cols = kept("vec_cols", [P, VEC_END - TS_ROW], F32)
+        vectors = kept("vectors", [P, PASS], BF16)
+        ln_rows = kept("ln_rows", [P, SLOTS, P], F32)
+        ln_weight = kept("ln_weight", [P, SLOTS, J_PASSES], F32)
+        vec_cols = kept("vec_cols", [P, END_ROW - SCALE_ROW], F32)
         one = kept("one", [P, 1], F32)
         vec_rows = kept("vec_rows", [P, P], F32)
-        gain_bc = [kept("gain_bc%d" % g, [P, PASS], BF16) for g in range(M_CHUNKS)]
-        c_codes = [kept("c_codes%d" % c, [P, K_PASSES, 2 * R_CHUNKS[c][1]], U8) for c in range(2)]
+        gain = [kept("gain%d" % g, [P, PASS], BF16) for g in range(M_CHUNKS)]
+        c_codes = [kept("c_codes%d" % part, [P, K_PASSES, 2 * R_PARTS[part][1]], U8) for part in (WIDE, NARROW)]
         c_plane = kept("c_plane", [P, K_PASSES, R], U8)
         h_plane_raw = kept("h_plane_raw", [P, K_PASSES, J], U8)
-        h_raw = [kept("h_raw%d" % a, [P, K_PASSES, 2 * PASS], U8) for a in range(J_PASSES)]
-        h_codes = [kept("h_codes%d" % a, [P, K_PASSES, 4, 2 * P], U8) for a in range(J_PASSES)]
-        h_plane = [kept("h_plane%d" % a, [P, K_PASSES, 4, P], U8) for a in range(J_PASSES)]
-        a_rows = {(a, g): kept("a_rows%d_%d" % (a, g), [P, 4, PASS], BF16) for a in range(J_PASSES) for g in range(M_CHUNKS)}
-        a_codes = {(a, g): kept("a_codes%d_%d" % (a, g), [P, PASS], U32) for a in range(J_PASSES) for g in range(M_CHUNKS)}
-        a_plane = {(a, g): kept("a_plane%d_%d" % (a, g), [P, PASS], U8) for a in range(J_PASSES) for g in range(M_CHUNKS)}
-        e_keys = [(a, 0) for a in range(J_PASSES)] + [(0, 1), (2, 1)]
-        e_rows = {k: kept("e_rows%d_%d" % k, [P, 4, PASS], BF16) for k in e_keys}
-        e_codes = {k: kept("e_codes%d_%d" % k, [P, PASS], U32) for k in e_keys}
-        e_plane = {k: kept("e_plane%d_%d" % k, [P, PASS], U8) for k in e_keys}
-
-        def e_place(a, c):
-            return ((a, 0), 0) if c == 0 else ((a - a % 2, 1), (a % 2) * R_CHUNKS[1][1])
-
+        h_loads = {0: 1, 1: 1, 2: 2}
+        h_sorts = {0: 1, 1: 3}
+        h_raw = {a0: kept("h_raw%d" % a0, [P, K_PASSES, 2 * PASS * n], U8) for a0, n in h_loads.items()}
+        h_codes = {a0: kept("h_codes%d" % a0, [P, n, K_PASSES, SLOTS, 2 * P], U8) for a0, n in h_loads.items()}
+        h_plane = {a0: kept("h_plane%d" % a0, [P, K_PASSES, n, SLOTS, P], U8) for a0, n in h_sorts.items()}
+        a_rows = {piece: kept("a_rows%d_%d" % piece, [P, SLOTS, PASS], BF16) for piece in pieces}
+        a_codes = {piece: kept("a_codes%d_%d" % piece, [P, PASS], U32) for piece in pieces}
+        a_plane = {piece: kept("a_plane%d_%d" % piece, [P, PASS], U8) for piece in pieces}
+        e_tiles = [(a, WIDE) for a in range(J_PASSES)] + [(0, NARROW), (2, NARROW)]
+        e_rows = {tile: kept("e_rows%d_%d" % tile, [P, SLOTS, PASS], BF16) for tile in e_tiles}
+        e_codes = {tile: kept("e_codes%d_%d" % tile, [P, PASS], U32) for tile in e_tiles}
+        e_plane = {tile: kept("e_plane%d_%d" % tile, [P, PASS], U8) for tile in e_tiles}
         y_codes = [kept("y_codes%d" % g, [P, R], U32) for g in range(M_CHUNKS)]
-        y_plane = [kept("y_plane%d" % g, [P, R], U8) for g in range(M_CHUNKS)]
+        base_last = kept("base_last", [P, PASS], F32)
+        y_plane = [kept("y_plane%d" % n, [P, R], U8) for n in range(2)]
 
-        nc.vector.memset(one[:], 1.0)
-        nc.vector.memset(h_plane_raw[:].rearrange("p g n -> p (g n)").bitcast(I32), 0)
-        nc.vector.memset(ident[:], 0.0)
-        nc.vector.memset(c_plane[:].rearrange("p g n -> p (g n)").bitcast(I32), 0)
-        nc.scalar.activation(out=rows[:].rearrange("p t n -> p (t n)"), in_=one[:].to_broadcast([P, PASS]), func=ACT.Ln)
+        def e_place(a, part):
+            if part == WIDE:
+                return (a, WIDE), 0
+            return (a - a % 2, NARROW), (a % 2) * R_PARTS[NARROW][1]
 
-        def load_plane(queue, plane, scales, quadrants):
+        vector.memset(one[:], 1.0)
+        vector.memset(h_plane_raw[:].rearrange("p g n -> p (g n)").bitcast(I32), 0)
+        vector.memset(ident[:], 0.0)
+        vector.memset(c_plane[:].rearrange("p g n -> p (g n)").bitcast(I32), 0)
+        scalar.activation(out=ln_rows[:].rearrange("p t n -> p (t n)"), in_=one[:].to_broadcast([P, PASS]), func=ACT.Ln)
+        make_identity(nc, ident[:], nomemset=True)
+
+        def load_plane(plane, scales, quadrants):
             for q in quadrants:
-                queue.dma_start(
+                nc.sync.dma_start(
                     out=plane[32 * q : 32 * q + 4, :, :].bitcast(I32),
                     in_=scales[:, 4 * q : 4 * q + 4, :].rearrange("g r n -> r g n").bitcast(I32),
                 )
 
-        def load_alleles(a, g):
-            dst = a_rows[a, g]
-            src = alleles[PASS * a : PASS * (a + 1), PASS * g : PASS * (g + 1)].rearrange("(s t i) m -> i s t m", t=4, i=4)
+        def load_piece(a, g):
+            src = alleles[PASS * a : PASS * (a + 1), PASS * g : PASS * (g + 1)].rearrange("(s t i) m -> i s t m", t=SLOTS, i=4)
             for i in range(4):
-                nc.sync.dma_start(out=dst[i:P:4, :, :], in_=src[i])
+                nc.sync.dma_start(out=a_rows[a, g][i:P:4, :, :], in_=src[i])
 
-        def load_h(a):
-            nc.sync.dma_start(
-                out=h_raw[a][:].bitcast(I32),
-                in_=h_words[:, :, 2 * PASS * a : 2 * PASS * (a + 1)].rearrange("g p n -> p g n").bitcast(I32),
-            )
+        def load_h(a0):
+            cols = slice(2 * PASS * a0, 2 * PASS * (a0 + h_loads[a0]))
+            nc.sync.dma_start(out=h_raw[a0][:].bitcast(I32), in_=h_words[:, :, cols].rearrange("g p n -> p g n").bitcast(I32))
 
-        def load_c(c):
-            r0, width = R_CHUNKS[c]
-            nc.sync.dma_start(
-                out=c_codes[c][:].bitcast(I32),
-                in_=c_words[:, :, 2 * r0 : 2 * (r0 + width)].rearrange("g p n -> p g n").bitcast(I32),
-            )
+        def load_c(part):
+            r0, width = R_PARTS[part]
+            cols = slice(2 * r0, 2 * (r0 + width))
+            nc.sync.dma_start(out=c_codes[part][:].bitcast(I32), in_=c_words[:, :, cols].rearrange("g p n -> p g n").bitcast(I32))
 
-        make_identity(nc, ident[:], nomemset=True)
-        nc.sync.dma_start(out=rows_bf[0:J_PASSES, :], in_=hap_weight.rearrange("(a n) -> a n", n=PASS))
-        load_alleles(0, 0)
-        load_plane(nc.sync, h_plane_raw, h_scales, (0,))
+        def load_gain(g):
+            nc.sync.dma_start(out=gain[g][:], in_=marker_gain[PASS * g : PASS * (g + 1)].partition_broadcast(P))
+
+        nc.sync.dma_start(out=vectors[0:J_PASSES, :], in_=hap_weight.rearrange("(a n) -> a n", n=PASS))
+        load_piece(0, 0)
+        load_plane(h_plane_raw, h_scales, (0,))
         load_h(0)
-        load_c(0)
-        load_plane(nc.sync, h_plane_raw, h_scales, (1, 2, 3))
-        load_plane(nc.sync, c_plane, c_scales, (0, 1, 2, 3))
+        load_c(WIDE)
+        load_plane(h_plane_raw, h_scales, (1, 2, 3))
+        load_plane(c_plane, c_scales, (0, 1, 2, 3))
         load_h(1)
-        load_alleles(1, 0)
+        load_piece(1, 0)
         load_h(2)
-        load_h(3)
-        load_alleles(2, 0)
-        nc.sync.dma_start(out=rows_bf[TS_ROW : TS_ROW + R_TILES, 0:P], in_=target_scale.rearrange("(a n) -> a n", n=P))
-        nc.sync.dma_start(out=rows_bf[BASE_ROW : BASE_ROW + M // P, 0:P], in_=base.rearrange("(a n) -> a n", n=P))
-        load_alleles(3, 0)
-        load_c(1)
-        nc.sync.dma_start(out=gain_bc[0][:], in_=marker_gain[0:PASS].partition_broadcast(P))
+        load_piece(2, 0)
+        nc.sync.dma_start(out=vectors[SCALE_ROW:BASE_ROW, 0:P], in_=target_scale.rearrange("(a n) -> a n", n=P))
+        nc.sync.dma_start(out=vectors[BASE_ROW:END_ROW, 0:P], in_=base.rearrange("(a n) -> a n", n=P))
+        load_piece(3, 0)
+        load_c(NARROW)
+        load_gain(0)
         for g in range(1, M_CHUNKS):
             for a in range(J_PASSES):
-                load_alleles(a, g)
-            nc.sync.dma_start(out=gain_bc[g][:], in_=marker_gain[PASS * g : PASS * (g + 1)].partition_broadcast(P))
+                load_piece(a, g)
+            load_gain(g)
 
         grouped = {}
 
-        def interleave(engine, key, src, tag=None, cols=slice(0, PASS)):
+        def interleave(engine, key, rows, cols, tag):
             if key not in grouped:
-                tag = tag or ("by_scalar" if engine is nc.scalar else "by_vector")
-                grouped[key] = work.tile([P, PASS, 4], BF16, name=tag, tag=tag, bufs=1 if tag == "by_gpsimd" else 3, align_bytes=64)
-            o = grouped[key][:, cols, :].rearrange("p (c i) t -> p c t i", i=4)
-            s = src[:, :, cols].rearrange("p t (c i) -> p c t i", i=4)
-            if engine is nc.scalar:
-                nc.scalar.copy(out=o, in_=s)
-            elif engine is nc.gpsimd:
-                nc.gpsimd.tensor_scalar(out=grouped[key][:, cols, :], in0=src[:, :, cols].rearrange("p t c -> p c t"), scalar1=1.0, scalar2=-0.0, op0=ALU.mult, op1=ALU.add)
+                bufs = 1 if tag == "for_gpsimd" else 3
+                grouped[key] = work.tile([P, PASS, SLOTS], BF16, name=tag, tag=tag, bufs=bufs, align_bytes=64)
+            dst, src = grouped[key][:, cols, :], rows[:, :, cols]
+            if engine is gpsimd:
+                gpsimd.tensor_scalar(
+                    out=dst, in0=src.rearrange("p t c -> p c t"), scalar1=1.0, scalar2=-0.0, op0=ALU.mult, op1=ALU.add
+                )
+                return
+            dst, src = dst.rearrange("p (c i) t -> p c t i", i=4), src.rearrange("p t (c i) -> p c t i", i=4)
+            if engine is scalar:
+                scalar.copy(out=dst, in_=src)
             else:
-                nc.vector.tensor_copy(out=o, in_=s)
+                vector.tensor_copy(out=dst, in_=src)
 
         def quantise(key, codes, plane):
-            nc.vector.quantize_mx(out=codes.bitcast(FP8X4), scales=plane, in_=grouped[key][:].rearrange("p c t -> p (c t)"))
+            vector.quantize_mx(out=codes.bitcast(FP8X4), scales=plane, in_=grouped[key][:].rearrange("p c t -> p (c t)"))
 
-        def al(engine, a, g, tag=None, cols=slice(0, PASS)):
-            src = a_rows[a, g][:]
-            interleave(engine, ("a", a, g), src, tag, cols)
+        def group_a(engine, piece, tag, cols=slice(0, PASS)):
+            interleave(engine, ("a", piece), a_rows[piece][:], cols, tag)
 
-        def qa(a, g):
-            quantise(("a", a, g), a_codes[a, g][:], a_plane[a, g][:])
+        def quantise_a(piece):
+            quantise(("a", piece), a_codes[piece][:], a_plane[piece][:])
 
-        def ei(a, c, engine=nc.vector, tag=None):
-            interleave(engine, ("e", a, c), e_rows[a, c][:], tag)
+        def group_e(engine, tile, tag):
+            interleave(engine, ("e", tile), e_rows[tile][:], slice(0, PASS), tag)
 
-        def qe(a, c):
-            quantise(("e", a, c), e_codes[a, c][:], e_plane[a, c][:])
+        def quantise_e(tile):
+            quantise(("e", tile), e_codes[tile][:], e_plane[tile][:])
 
-        def sort_h(a):
-            nc.vector.tensor_copy(
-                out=h_codes[a][:].bitcast(I32).rearrange("p g t (s e) -> p g t s e", e=2),
-                in_=h_raw[a][:].bitcast(I32).rearrange("p g (s t e) -> p g t s e", t=4, e=2),
+        def h_place(a, starts):
+            a0 = max(start for start in starts if start <= a)
+            return a0, a - a0
+
+        def sort_h_words(a):
+            a0, n = h_place(a, h_loads)
+            vector.tensor_copy(
+                out=h_codes[a0][:, n].bitcast(I32).rearrange("p g t (s e) -> p g t s e", e=2),
+                in_=h_raw[a0][:, :, 2 * PASS * n : 2 * PASS * (n + 1)].bitcast(I32).rearrange("p g (s t e) -> p g t s e", t=SLOTS, e=2),
             )
-            nc.vector.tensor_copy(
-                out=h_plane[a][:].bitcast(I32),
-                in_=h_plane_raw[:, :, PASS * a : PASS * (a + 1)].bitcast(I32).rearrange("p g (s t) -> p g t s", t=4),
+
+        def sort_h_plane(a0):
+            cols = slice(PASS * a0, PASS * (a0 + h_sorts[a0]))
+            vector.tensor_copy(
+                out=h_plane[a0][:].bitcast(I32),
+                in_=h_plane_raw[:, :, cols].bitcast(I32).rearrange("p g (a s t) -> p g a t s", t=SLOTS, a=h_sorts[a0]),
             )
 
-        def emission(a, c):
-            r0, width = R_CHUNKS[c]
-            key, off = e_place(a, c)
-            for t in range(4):
-                bank = psum.tile([P, PASS], F32, name="s_bank", tag="mx_bank", bufs=4)
+        def emission(a, part):
+            r0, width = R_PARTS[part]
+            tile, col0 = e_place(a, part)
+            words0, words_n = h_place(a, h_loads)
+            plane0, plane_n = h_place(a, h_sorts)
+            for t in range(SLOTS):
+                bank = mx_bank()
                 for g in range(K_PASSES):
                     nc.tensor.matmul_mx(
                         out=bank[:, 0:width],
-                        lhsT=h_codes[a][:, g, t, :].bitcast(FP4X4),
-                        lhsT_scale=h_plane[a][:, g, t, :],
-                        rhs=c_codes[c][:, g, :].bitcast(FP4X4),
+                        lhsT=h_codes[words0][:, words_n, g, t, :].bitcast(FP4X4),
+                        lhsT_scale=h_plane[plane0][:, g, plane_n, t, :],
+                        rhs=c_codes[part][:, g, :].bitcast(FP4X4),
                         rhs_scale=c_plane[:, g, r0 : r0 + width],
                         start=(g == 0),
                         stop=(g == K_PASSES - 1),
                     )
-                nc.scalar.activation(out=e_rows[key][:, t, off : off + width], in_=bank[:, 0:width], func=ACT.Exp, bias=ln_w[:, t, a : a + 1])
-
-        base_bank, d_of, z_of, y_of, yb_of, tb_of, yg_of = {}, {}, {}, {}, {}, {}, {}
-
-        def product(n, passes=range(J_PASSES)):
-            g, rt = divmod(n, R_TILES)
-            c = 0 if rt < 4 else 1
-            if n not in d_of:
-                d_of[n] = psum.tile([P, PASS], F32, name="d_bank", tag="mx_bank", bufs=4)
-            for a in passes:
-                key, off = e_place(a, c)
-                cols = slice(off + P * rt - R_CHUNKS[c][0], off + P * (rt + 1) - R_CHUNKS[c][0])
-                nc.tensor.matmul_mx(
-                    out=d_of[n][:],
-                    lhsT=e_codes[key][:, cols].bitcast(FP8X4),
-                    lhsT_scale=e_plane[key][:, cols],
-                    rhs=a_codes[a, g][:].bitcast(FP8X4),
-                    rhs_scale=a_plane[a, g][:],
-                    start=(a == 0),
-                    stop=(a == J_PASSES - 1),
+                scalar.activation(
+                    out=e_rows[tile][:, t, col0 : col0 + width], in_=bank[:, 0:width], func=ACT.Exp, bias=ln_weight[:, t, a : a + 1]
                 )
 
-        def scale_d(n):
-            g, rt = divmod(n, R_TILES)
-            if n % 2 == 0:
-                z_of[n // 2] = work.tile([P, 2, PASS], F32, name="z", tag="z", bufs=2)
-            nc.vector.scalar_tensor_tensor(
-                out=z_of[n // 2][:, n % 2, :], in0=d_of[n][:], scalar=vec_cols[:, rt : rt + 1], in1=gain_bc[g][:],
-                op0=ALU.mult, op1=ALU.mult,
+        base_bank, d_bank, z_of, y_of, rounded, turned, y_grouped = {}, {}, {}, {}, {}, {}, {}
+
+        def place(pair, h):
+            g, k = divmod(pair, PAIRS_PER_CHUNK)
+            return g, 2 * k + h
+
+        def product(pair, h, a):
+            g, rt = place(pair, h)
+            part = WIDE if P * rt < R_PARTS[NARROW][0] else NARROW
+            if a == 0:
+                d_bank[pair, h] = mx_bank()
+            tile, col0 = e_place(a, part)
+            first = col0 + P * rt - R_PARTS[part][0]
+            nc.tensor.matmul_mx(
+                out=d_bank[pair, h][:],
+                lhsT=e_codes[tile][:, first : first + P].bitcast(FP8X4),
+                lhsT_scale=e_plane[tile][:, first : first + P],
+                rhs=a_codes[a, g][:].bitcast(FP8X4),
+                rhs_scale=a_plane[a, g][:],
+                start=(a == 0),
+                stop=(a == J_PASSES - 1),
+            )
+
+        def scale_d(pair, h):
+            g, rt = place(pair, h)
+            if h == 0:
+                z_of[pair] = work.tile([P, 2, PASS], F32, name="z", tag="z", bufs=2)
+            vector.scalar_tensor_tensor(
+                out=z_of[pair][:, h, :],
+                in0=d_bank[pair, h][:],
+                scalar=vec_cols[:, rt : rt + 1],
+                in1=gain[g][:],
+                op0=ALU.mult,
+                op1=ALU.mult,
             )
 
         def spread_base(g):
-            bank = psum.tile([P, PASS], F32, name="b_bank", tag="b_bank", bufs=2)
-            base_bank[g] = bank
-            for c in range(4):
-                nc.tensor.transpose(bank[:, P * c : P * (c + 1)], vec_cols[:, R_TILES + 4 * g + c : R_TILES + 4 * g + c + 1].to_broadcast([P, P]), ident[:])
+            base_bank[g] = psum.tile([P, PASS], F32, name="base_bank", tag="base_bank", bufs=2)
+            for c in range(PASS // P):
+                col = R_TILES + (PASS // P) * g + c
+                nc.tensor.transpose(base_bank[g][:, P * c : P * (c + 1)], vec_cols[:, col : col + 1].to_broadcast([P, P]), ident[:])
 
-        def finish(pair, h0, h1):
-            g, k = divmod(pair, R_TILES // 2)
-            if h0 == 0:
+        def add_base(engine, pair, h0, h1):
+            if pair not in y_of:
                 y_of[pair] = work.tile([P, 2, PASS], F32, name="y", tag="y", bufs=4)
-            y = y_of[pair][:, h0:h1, :]
-            nc.vector.tensor_tensor(
-                out=y, in0=z_of[pair][:, h0:h1, :], in1=base_bank[g][:].unsqueeze(1).to_broadcast([P, h1 - h0, PASS]), op=ALU.add
-            )
-            rows_out = out_0[P * (2 * k + h0) : P * (2 * k + h1), PASS * g : PASS * (g + 1)]
-            nc.sync.dma_start(out=rows_out.rearrange("(h r) m -> r h m", r=P), in_=y)
-
-        def round_y(pair, h0, h1, engine):
-            if h0 == 0:
-                yb_of[pair] = work.tile([P, 2, 2, P, 2], BF16, name="yb", tag="yb", bufs=2, align_bytes=64)
-            src = y_of[pair][:, h0:h1, :].rearrange("r h (p u e) -> r h u p e", u=2, e=2)
-            if engine is nc.scalar:
-                nc.scalar.copy(out=yb_of[pair][:, h0:h1], in_=src)
-            else:
-                nc.vector.tensor_copy(out=yb_of[pair][:, h0:h1], in_=src)
-
-        def turn(pair, h0, h1):
-            bank = psum.tile([P, 2, 2, P], F32, name="t_bank", tag="t_bank", bufs=2)
-            tb_of[pair, h0] = bank
-            for h in range(h0, h1):
-                words = yb_of[pair][:, h].rearrange("r u p e -> r (u p e)").bitcast(F32)
-                for u in range(2):
-                    nc.tensor.transpose(bank[:, h - h0, u, :], words[:, P * u : P * (u + 1)], ident[:])
-
-        def leave(pair, h0, h1):
-            yg = work.tile([P, (h1 - h0) * P * 4], BF16, name="yg", tag="yg", bufs=4, align_bytes=64)
-            yg_of[pair, h0] = yg
-            nc.scalar.copy(
-                out=yg[:].bitcast(F32).rearrange("p (h r u) -> p h r u", r=P, u=2),
-                in_=tb_of[pair, h0][:, 0 : h1 - h0].rearrange("p h u r -> p h r u"),
+            spread = base_last if engine is gpsimd else base_bank[pair // PAIRS_PER_CHUNK]
+            engine.tensor_tensor(
+                out=y_of[pair][:, h0:h1, :],
+                in0=z_of[pair][:, h0:h1, :],
+                in1=spread[:].unsqueeze(1).to_broadcast([P, h1 - h0, PASS]),
+                op=ALU.add,
             )
 
-        def planes(pair, h0, h1):
-            g, k = divmod(pair, R_TILES // 2)
-            cols = slice(P * (2 * k + h0), P * (2 * k + h1))
-            nc.vector.quantize_mx(out=y_codes[g][:, cols].bitcast(FP8X4), scales=y_plane[g][:, cols], in_=yg_of[pair, h0][:])
-            if cols.stop == R or (pair, h1) == (last, 1):
-                done = slice(R - P if (pair, h0) == (last, 1) else 0, cols.stop)
-                nc.sync.dma_start(out=out_1[g, :, done, :].rearrange("p m t -> p (m t)").bitcast(I32), in_=y_codes[g][:, done].bitcast(I32))
-            if cols.stop == R:
-                queue = nc.scalar if g == M_CHUNKS - 1 else nc.sync
-                for q in range(4):
-                    queue.dma_start(out=out_2[g, 4 * q : 4 * q + 4, :].bitcast(I32), in_=y_plane[g][32 * q : 32 * q + 4, :].bitcast(I32))
+        def store_y(pair, h0, h1):
+            g, rt = place(pair, h0)
+            dst = out_0[P * rt : P * (rt + h1 - h0), PASS * g : PASS * (g + 1)]
+            nc.sync.dma_start(out=dst.rearrange("(h r) m -> r h m", r=P), in_=y_of[pair][:, h0:h1, :])
 
-        nc.scalar.activation(
-            out=rows[0:J_PASSES, :, :].rearrange("a t (s i) -> a t s i", i=4),
-            in_=rows_bf[0:J_PASSES, :].rearrange("a (s t i) -> a t s i", t=4, i=4),
+        def by_word(ap):
+            return ap.rearrange("r (p u e) -> r u p e", u=2, e=2)
+
+        def open_rounded(pair):
+            rounded[pair] = work.tile([P, 2, 2, P, 2], BF16, name="rounded", tag="rounded", bufs=3, align_bytes=64)
+
+        def round_y(pair):
+            open_rounded(pair)
+            scalar.copy(out=rounded[pair][:], in_=y_of[pair][:].rearrange("r h (p u e) -> r h u p e", u=2, e=2))
+
+        def turn(pair):
+            turned[pair] = turn_bank()
+            words = rounded[pair][:].rearrange("r h u p e -> r (h u p e)").bitcast(F32)
+            for c in range(PASS // P):
+                nc.tensor.transpose(turned[pair][:, P * c : P * (c + 1)], words[:, P * c : P * (c + 1)], ident[:])
+
+        def group_y(pair):
+            y_grouped[pair] = work.tile([P, 2 * P * SLOTS], BF16, name="y_grouped", tag="y_grouped", bufs=4, align_bytes=64)
+            scalar.copy(
+                out=y_grouped[pair][:].bitcast(F32).rearrange("p (h r u) -> p h r u", h=2, u=2),
+                in_=turned[pair][:].rearrange("p (h u r) -> p h r u", h=2, u=2),
+            )
+
+        def planes(pair):
+            g, rt = place(pair, 0)
+            cols = slice(P * rt, P * (rt + 2))
+            plane = y_plane[min(g, 1)]
+            vector.quantize_mx(out=y_codes[g][:, cols].bitcast(FP8X4), scales=plane[4 * max(g - 1, 0) : P, cols], in_=y_grouped[pair][:])
+            nc.sync.dma_start(out=out_1[g, :, cols, :].rearrange("p m t -> p (m t)").bitcast(I32), in_=y_codes[g][:, cols].bitcast(I32))
+
+        def store_plane(queue, plane, g0, g1):
+            for q in range(4):
+                queue.dma_start(
+                    out=out_2[g0:g1, 4 * q : 4 * q + 4, :].bitcast(I32),
+                    in_=plane[32 * q : 32 * q + 4 * (g1 - g0), :].bitcast(I32),
+                )
+
+        scalar.activation(
+            out=ln_rows[0:J_PASSES, :, :].rearrange("a t (s i) -> a t s i", i=4),
+            in_=vectors[0:J_PASSES, :].rearrange("a (s t i) -> a t s i", t=SLOTS, i=4),
             func=ACT.Ln,
         )
-        nc.scalar.activation(out=vec_rows[:], in_=one[:].to_broadcast([P, P]), func=ACT.Exp)
-        al(nc.vector, 0, 0)
-        col_bank = psum.tile([P, 4, P], F32, name="t_bank", tag="t_bank", bufs=2)
-        for t in range(4):
-            nc.tensor.transpose(col_bank[:, t, :], rows[:, t, :], ident[:])
-        nc.vector.tensor_copy(out=ln_w[:], in_=col_bank[:, :, 0:J_PASSES])
-        qa(0, 0)
-        sort_h(0)
+        scalar.activation(out=vec_rows[:], in_=one[:].to_broadcast([P, P]), func=ACT.Exp)
+        group_a(vector, (0, 0), "for_vector")
+        ln_bank = turn_bank()
+        for t in range(SLOTS):
+            nc.tensor.transpose(ln_bank[:, P * t : P * (t + 1)], ln_rows[:, t, :], ident[:])
+        vector.tensor_copy(out=ln_weight[:], in_=ln_bank[:].rearrange("p (t n) -> p t n", t=SLOTS)[:, :, 0:J_PASSES])
+        quantise_a((0, 0))
+        sort_h_words(0)
+        sort_h_plane(0)
+        sort_h_plane(1)
 
-        emission(0, 0)
-        sort_h(1)
-        al(nc.vector, 1, 0)
-        sort_h(2)
-        qa(1, 0)
-        emission(1, 0)
-        ei(0, 0)
-        sort_h(3)
-        qe(0, 0)
-        emission(2, 0)
-        al(nc.vector, 2, 0)
-        ei(1, 0)
-        nc.vector.tensor_copy(out=vec_rows[TS_ROW:VEC_END, :], in_=rows_bf[TS_ROW:VEC_END, 0:P])
-        qa(2, 0)
-        qe(1, 0)
-        emission(3, 0)
-        V, S, G = nc.vector, nc.scalar, nc.gpsimd
-        mine, rest = slice(0, G_COLS), slice(G_COLS, PASS)
-        ts_bank = psum.tile([P, 4, P], F32, name="t_bank", tag="t_bank", bufs=2)
-        nc.tensor.transpose(ts_bank[:, 0, :], vec_rows[:], ident[:])
-        nc.vector.tensor_copy(out=vec_cols[:], in_=ts_bank[:, 0, TS_ROW:VEC_END])
-        al(V, 3, 0)
-        ei(2, 0)
-        qa(3, 0)
-        emission(0, 1)
+        emission(0, WIDE)
+        sort_h_words(1)
+        group_a(vector, (1, 0), "for_vector")
+        sort_h_words(2)
+        quantise_a((1, 0))
+        emission(1, WIDE)
+        group_e(vector, (0, WIDE), "for_vector")
+        sort_h_words(3)
+        quantise_e((0, WIDE))
+        emission(2, WIDE)
+        group_a(vector, (2, 0), "for_vector")
+        group_e(vector, (1, WIDE), "for_vector")
+        vector.tensor_copy(out=vec_rows[SCALE_ROW:END_ROW, :], in_=vectors[SCALE_ROW:END_ROW, 0:P])
+        quantise_a((2, 0))
+        quantise_e((1, WIDE))
+        emission(3, WIDE)
+        vec_bank = turn_bank()
+        nc.tensor.transpose(vec_bank[:, 0:P], vec_rows[:], ident[:])
+        vector.tensor_copy(out=vec_cols[:], in_=vec_bank[:, SCALE_ROW:END_ROW])
+        group_a(vector, (3, 0), "for_vector")
+        group_e(vector, (2, WIDE), "for_vector")
+        quantise_a((3, 0))
+
+        emission(0, NARROW)
         spread_base(0)
-        emission(1, 1)
-        ei(3, 0)
-        qe(2, 0)
-        emission(2, 1)
-        emission(3, 1)
-        qe(3, 0)
-        ei(0, 1, V, "by_gpsimd")
-        between = {0: [lambda: qe(0, 1), lambda: al(G, 1, 1, "by_gpsimd", mine)]}
-        after = {}
-        vector_extra = {
-            1: [lambda: qe(2, 1), lambda: qa(0, 1), lambda: qa(1, 1), lambda: al(G, 3, 1, "by_gpsimd", mine)],
-            2: [lambda: qa(2, 1), lambda: qa(3, 1), lambda: al(G, 0, 2, "by_gpsimd", mine)],
-            3: [lambda: qa(0, 2), lambda: al(G, 2, 2, "by_gpsimd", mine)],
-            4: [lambda: qa(1, 2), lambda: qa(2, 2), lambda: al(G, 3, 2, "by_gpsimd", mine)],
-            5: [lambda: qa(3, 2)],
-        }
-        scalar_extra = {
-            0: [lambda: ei(2, 1, S), lambda: al(S, 0, 1)],
-            1: [lambda: al(S, 1, 1, None, rest)],
-            2: [lambda: al(S, 3, 1, None, rest)],
-            3: [lambda: al(S, 0, 2, None, rest)],
-            4: [lambda: al(S, 2, 2, None, rest)],
-            5: [lambda: al(S, 3, 2, None, rest)],
-        }
-        pairs = M_CHUNKS * R_TILES // 2
-        last = pairs - 1
-        LR, LT, LL, LP = 1, 2, 2, 3
-        for k in range(pairs):
-            if k < pairs:
-                if k < last:
-                    for a in range(J_PASSES):
-                        product(2 * k, [a])
-                        product(2 * k + 1, [a])
-                else:
-                    product(2 * k)
-                    product(2 * k + 1)
-                scale_d(2 * k)
-                for step in between.get(k, []):
-                    step()
-                if k < last:
-                    scale_d(2 * k + 1)
-            for step in after.get(k, []):
-                step()
-            if 0 <= k - LT < pairs:
-                turn(k - LT, 0, 2)
-            if k in (2, 4):
-                spread_base(k // 2)
-            for step in scalar_extra.get(k, []):
-                step()
-            if 0 <= k - LR < last:
-                round_y(k - LR, 0, 2, S)
-            if 0 <= k - LL < pairs:
-                leave(k - LL, 0, 2)
-            if k in (1, 3):
-                al(S, 2 if k == 1 else 1, 1 if k == 1 else 2)
-            if 0 <= k - LP < pairs:
-                planes(k - LP, 0, 2)
-            for step in vector_extra.get(k, []):
-                step()
-            if k < last:
-                finish(k, 0, 2)
-        finish(last, 0, 1)
-        round_y(last, 0, 1, S)
-        scale_d(2 * last + 1)
-        nc.vector.tensor_tensor(
-            out=yb_of[last][:, 1],
-            in0=z_of[last][:, 1, :].rearrange("r (p u e) -> r u p e", u=2, e=2),
-            in1=base_bank[M_CHUNKS - 1][:].rearrange("r (p u e) -> r u p e", u=2, e=2),
-            op=ALU.add,
+        emission(1, NARROW)
+        group_e(vector, (3, WIDE), "for_vector")
+        quantise_e((2, WIDE))
+        emission(2, NARROW)
+        emission(3, NARROW)
+        quantise_e((3, WIDE))
+        group_e(vector, (0, NARROW), "for_gpsimd")
+        group_a(vector, (0, 1), "for_scalar", slice(0, VECTOR_COLS))
+
+        later = [(a, g) for g in range(1, M_CHUNKS) for a in range(J_PASSES)]
+        quantised = 0
+
+        def start_gpsimd(pair):
+            group_a(gpsimd, GPSIMD_PIECES[pair], "for_gpsimd", slice(0, GPSIMD_COLS))
+
+        for pair in range(LAST):
+            for a in range(J_PASSES):
+                product(pair, 0, a)
+                product(pair, 1, a)
+            scale_d(pair, 0)
+            if pair >= LAST_CHUNK_START:
+                add_base(gpsimd, pair, 0, 1)
+            if pair == 0:
+                quantise_e((0, NARROW))
+                start_gpsimd(0)
+            scale_d(pair, 1)
+            if pair >= 2:
+                turn(pair - 2)
+            if pair in (2, 4):
+                spread_base(pair // 2)
+
+            if pair == 0:
+                group_e(scalar, (2, NARROW), "for_scalar")
+                group_a(scalar, (0, 1), "for_scalar", slice(VECTOR_COLS, PASS))
+            elif pair <= len(GPSIMD_PIECES):
+                group_a(scalar, GPSIMD_PIECES[pair - 1], "for_gpsimd", slice(GPSIMD_COLS, PASS))
+            if pair >= 1:
+                round_y(pair - 1)
+            if pair >= 2:
+                group_y(pair - 2)
+            if pair == LAST_CHUNK_START - 1:
+                scalar.copy(out=base_last[:], in_=base_bank[M_CHUNKS - 1][:])
+            if 1 <= pair < len(GPSIMD_PIECES):
+                between = later[later.index(GPSIMD_PIECES[pair - 1]) + 1 : later.index(GPSIMD_PIECES[pair])]
+                for piece in between:
+                    group_a(scalar, piece, "for_scalar")
+
+            if pair < LAST_CHUNK_START:
+                if pair >= 3:
+                    planes(pair - 3)
+                if pair == PAIRS_PER_CHUNK + 2:
+                    store_plane(nc.sync, y_plane[0], 0, 1)
+                if pair == 1:
+                    quantise_e((2, NARROW))
+                if pair >= 1:
+                    due = later.index(GPSIMD_PIECES[pair - 1]) + 1
+                    for piece in later[quantised:due]:
+                        quantise_a(piece)
+                    quantised = due
+                if 1 <= pair < len(GPSIMD_PIECES):
+                    start_gpsimd(pair)
+                add_base(vector, pair, 0, 2)
+                store_y(pair, 0, 2)
+            else:
+                add_base(vector, pair, 1, 2)
+                store_y(pair, 0, 2)
+                if pair == LAST_CHUNK_START:
+                    planes(pair - 3)
+                planes(pair - 2)
+
+        for h in range(2):
+            for a in range(J_PASSES):
+                product(LAST, h, a)
+        scale_d(LAST, 0)
+        add_base(vector, LAST, 0, 1)
+        store_y(LAST, 0, 1)
+        open_rounded(LAST)
+        gpsimd.tensor_scalar(
+            out=rounded[LAST][:, 0], in0=by_word(y_of[LAST][:, 0, :]), scalar1=1.0, scalar2=-0.0, op0=ALU.mult, op1=ALU.add
         )
-        finish(last, 1, 2)
-        turn(last - 1, 0, 2)
-        leave(last - 1, 0, 2)
-        turn(last, 0, 1)
-        leave(last, 0, 1)
-        planes(last - 2, 0, 2)
-        planes(last - 1, 0, 2)
-        turn(last, 1, 2)
-        leave(last, 1, 2)
-        planes(last, 0, 1)
-        planes(last, 1, 2)
+        scale_d(LAST, 1)
+        turn(LAST - 2)
+        round_y(LAST - 1)
+        group_y(LAST - 2)
+        vector.tensor_tensor(
+            out=rounded[LAST][:, 1], in0=by_word(z_of[LAST][:, 1, :]), in1=by_word(base_bank[M_CHUNKS - 1][:]), op=ALU.add
+        )
+        add_base(vector, LAST, 1, 2)
+        store_y(LAST, 1, 2)
+        planes(LAST - 2)
+        for pair in (LAST - 1, LAST):
+            turn(pair)
+            group_y(pair)
+        for pair in (LAST - 1, LAST):
+            planes(pair)
+        store_plane(scalar, y_plane[1], 1, M_CHUNKS)

@@ -26,7 +26,6 @@ R_TILES = R // P
 PAIRS_PER_CHUNK = R_TILES // 2
 PAIRS = M_CHUNKS * PAIRS_PER_CHUNK
 LAST = PAIRS - 1
-LAST_CHUNK_START = PAIRS - PAIRS_PER_CHUNK
 
 WIDE, NARROW = 0, 1
 R_PARTS = ((0, 512), (512, 256))
@@ -36,8 +35,7 @@ BASE_ROW = SCALE_ROW + R_TILES
 END_ROW = BASE_ROW + M // P
 
 GPSIMD_PIECES = ((1, 1), (3, 1), (0, 2), (2, 2), (3, 2))
-GPSIMD_COLS = 320
-VECTOR_COLS = 256
+GPSIMD_COLS = 352
 
 
 def tile_haplotype_emission_alleles_k5_kernel(
@@ -85,7 +83,6 @@ def tile_haplotype_emission_alleles_k5_kernel(
         e_codes = {tile: kept("e_codes%d_%d" % tile, [P, PASS], U32) for tile in e_tiles}
         e_plane = {tile: kept("e_plane%d_%d" % tile, [P, PASS], U8) for tile in e_tiles}
         y_codes = [kept("y_codes%d" % g, [P, R], U32) for g in range(M_CHUNKS)]
-        base_last = kept("base_last", [P, PASS], F32)
         y_plane = [kept("y_plane%d" % n, [P, R], U8) for n in range(2)]
 
         def e_place(a, part):
@@ -259,19 +256,16 @@ def tile_haplotype_emission_alleles_k5_kernel(
                 col = R_TILES + (PASS // P) * g + c
                 nc.tensor.transpose(base_bank[g][:, P * c : P * (c + 1)], vec_cols[:, col : col + 1].to_broadcast([P, P]), ident[:])
 
-        def add_base(engine, pair, h0, h1):
-            if pair not in y_of:
+        def add_base(pair, h0, h1):
+            if h0 == 0:
                 y_of[pair] = work.tile([P, 2, PASS], F32, name="y", tag="y", bufs=4)
-            spread = base_last if engine is gpsimd else base_bank[pair // PAIRS_PER_CHUNK]
-            engine.tensor_tensor(
+            g, rt = place(pair, h0)
+            vector.tensor_tensor(
                 out=y_of[pair][:, h0:h1, :],
                 in0=z_of[pair][:, h0:h1, :],
-                in1=spread[:].unsqueeze(1).to_broadcast([P, h1 - h0, PASS]),
+                in1=base_bank[g][:].unsqueeze(1).to_broadcast([P, h1 - h0, PASS]),
                 op=ALU.add,
             )
-
-        def store_y(pair, h0, h1):
-            g, rt = place(pair, h0)
             dst = out_0[P * rt : P * (rt + h1 - h0), PASS * g : PASS * (g + 1)]
             nc.sync.dma_start(out=dst.rearrange("(h r) m -> r h m", r=P), in_=y_of[pair][:, h0:h1, :])
 
@@ -360,7 +354,6 @@ def tile_haplotype_emission_alleles_k5_kernel(
         emission(3, NARROW)
         quantise_e((3, WIDE))
         group_e(vector, (0, NARROW), "for_gpsimd")
-        group_a(vector, (0, 1), "for_scalar", slice(0, VECTOR_COLS))
 
         later = [(a, g) for g in range(1, M_CHUNKS) for a in range(J_PASSES)]
         quantised = 0
@@ -373,8 +366,6 @@ def tile_haplotype_emission_alleles_k5_kernel(
                 product(pair, 0, a)
                 product(pair, 1, a)
             scale_d(pair, 0)
-            if pair >= LAST_CHUNK_START:
-                add_base(gpsimd, pair, 0, 1)
             if pair == 0:
                 quantise_e((0, NARROW))
                 start_gpsimd(0)
@@ -386,49 +377,39 @@ def tile_haplotype_emission_alleles_k5_kernel(
 
             if pair == 0:
                 group_e(scalar, (2, NARROW), "for_scalar")
-                group_a(scalar, (0, 1), "for_scalar", slice(VECTOR_COLS, PASS))
+                group_a(scalar, later[0], "for_scalar")
             elif pair <= len(GPSIMD_PIECES):
                 group_a(scalar, GPSIMD_PIECES[pair - 1], "for_gpsimd", slice(GPSIMD_COLS, PASS))
             if pair >= 1:
                 round_y(pair - 1)
             if pair >= 2:
                 group_y(pair - 2)
-            if pair == LAST_CHUNK_START - 1:
-                scalar.copy(out=base_last[:], in_=base_bank[M_CHUNKS - 1][:])
             if 1 <= pair < len(GPSIMD_PIECES):
                 between = later[later.index(GPSIMD_PIECES[pair - 1]) + 1 : later.index(GPSIMD_PIECES[pair])]
                 for piece in between:
                     group_a(scalar, piece, "for_scalar")
 
-            if pair < LAST_CHUNK_START:
-                if pair >= 3:
-                    planes(pair - 3)
-                if pair == PAIRS_PER_CHUNK + 2:
-                    store_plane(nc.sync, y_plane[0], 0, 1)
-                if pair == 1:
-                    quantise_e((2, NARROW))
-                if pair >= 1:
-                    due = later.index(GPSIMD_PIECES[pair - 1]) + 1
-                    for piece in later[quantised:due]:
-                        quantise_a(piece)
-                    quantised = due
-                if 1 <= pair < len(GPSIMD_PIECES):
-                    start_gpsimd(pair)
-                add_base(vector, pair, 0, 2)
-                store_y(pair, 0, 2)
-            else:
-                add_base(vector, pair, 1, 2)
-                store_y(pair, 0, 2)
-                if pair == LAST_CHUNK_START:
-                    planes(pair - 3)
-                planes(pair - 2)
+            if pair >= 3:
+                planes(pair - 3)
+            if pair - 3 == PAIRS_PER_CHUNK - 1:
+                store_plane(nc.sync, y_plane[0], 0, 1)
+            if pair == 1:
+                quantise_e((2, NARROW))
+            if 1 <= pair <= len(GPSIMD_PIECES):
+                due = later.index(GPSIMD_PIECES[pair - 1]) + 1
+                for piece in later[quantised:due]:
+                    quantise_a(piece)
+                quantised = due
+            if 1 <= pair < len(GPSIMD_PIECES):
+                start_gpsimd(pair)
+            add_base(pair, 0, 2)
 
         for h in range(2):
             for a in range(J_PASSES):
                 product(LAST, h, a)
         scale_d(LAST, 0)
-        add_base(vector, LAST, 0, 1)
-        store_y(LAST, 0, 1)
+        planes(LAST - 3)
+        add_base(LAST, 0, 1)
         open_rounded(LAST)
         gpsimd.tensor_scalar(
             out=rounded[LAST][:, 0], in0=by_word(y_of[LAST][:, 0, :]), scalar1=1.0, scalar2=-0.0, op0=ALU.mult, op1=ALU.add
@@ -440,8 +421,7 @@ def tile_haplotype_emission_alleles_k5_kernel(
         vector.tensor_tensor(
             out=rounded[LAST][:, 1], in0=by_word(z_of[LAST][:, 1, :]), in1=by_word(base_bank[M_CHUNKS - 1][:]), op=ALU.add
         )
-        add_base(vector, LAST, 1, 2)
-        store_y(LAST, 1, 2)
+        add_base(LAST, 1, 2)
         planes(LAST - 2)
         for pair in (LAST - 1, LAST):
             turn(pair)

from contextlib import ExitStack

import concourse.mybir as mybir
from concourse.masks import make_identity

R, K, J, M = 768, 1024, 2048, 1536
FLOPS = 2 * R * K * J + 2 * R * J * M

F32 = mybir.dt.float32
BF16 = mybir.dt.bfloat16
I32 = mybir.dt.int32
U32 = mybir.dt.uint32
U8 = mybir.dt.uint8
FP8X4 = mybir.dt.float8_e4m3fn_x4
FP4X4 = mybir.dt.float4_e2m1fn_x4
ACT = mybir.ActivationFunctionType
ALU = mybir.AluOpType

P = 128
SLOTS = 4
PASS = P * SLOTS
K_PASSES = K // PASS
J_PASSES = J // PASS
M_CHUNKS = M // PASS
R_TILES = R // P
PAIRS_PER_CHUNK = R_TILES // 2
PAIRS = M_CHUNKS * PAIRS_PER_CHUNK
LAST = PAIRS - 1

WIDE, NARROW = 0, 1
R_PARTS = ((0, 512), (512, 256))

SCALE_ROW = 64
BASE_ROW = SCALE_ROW + R_TILES
END_ROW = BASE_ROW + M // P

GPSIMD_PIECES = ((1, 1), (3, 1), (0, 2), (2, 2), (3, 2))
GPSIMD_COLS = 352


def tile_haplotype_emission_alleles_k5_kernel(
    tc, c_words, c_scales, h_words, h_scales, hap_weight, alleles, target_scale, marker_gain, base, out_0, out_1, out_2
):
    nc = tc.nc
    vector, scalar, gpsimd = nc.vector, nc.scalar, nc.gpsimd
    with ExitStack() as ctx:
        keep = ctx.enter_context(tc.tile_pool(name="keep", bufs=1))
        work = ctx.enter_context(tc.tile_pool(name="work", bufs=1))
        psum = ctx.enter_context(tc.psum_pool(name="psum", bufs=1))
        ctx.enter_context(tc.manual_schedule())

        def kept(name, shape, dtype):
            return keep.tile(shape, dtype, name=name, align_bytes=64)

        def mx_bank():
            return psum.tile([P, PASS], F32, name="mx_bank", tag="mx_bank", bufs=4)

        def turn_bank():
            return psum.tile([P, PASS], F32, name="turn_bank", tag="turn_bank", bufs=2)

        pieces = [(a, g) for a in range(J_PASSES) for g in range(M_CHUNKS)]
        ident = kept("ident", [P, P], F32)
        vectors = kept("vectors", [P, PASS], BF16)
        ln_rows = kept("ln_rows", [P, SLOTS, P], F32)
        ln_weight = kept("ln_weight", [P, SLOTS, J_PASSES], F32)
        vec_cols = kept("vec_cols", [P, END_ROW - SCALE_ROW], F32)
        one = kept("one", [P, 1], F32)
        vec_rows = kept("vec_rows", [P, P], F32)
        gain = [kept("gain%d" % g, [P, PASS], BF16) for g in range(M_CHUNKS)]
        c_codes = [kept("c_codes%d" % part, [P, K_PASSES, 2 * R_PARTS[part][1]], U8) for part in (WIDE, NARROW)]
        c_plane = kept("c_plane", [P, K_PASSES, R], U8)
        h_plane_raw = kept("h_plane_raw", [P, K_PASSES, J], U8)
        h_loads = {0: 1, 1: 1, 2: 2}
        h_sorts = {0: 1, 1: 3}
        h_raw = {a0: kept("h_raw%d" % a0, [P, K_PASSES, 2 * PASS * n], U8) for a0, n in h_loads.items()}
        h_codes = {a0: kept("h_codes%d" % a0, [P, n, K_PASSES, SLOTS, 2 * P], U8) for a0, n in h_loads.items()}
        h_plane = {a0: kept("h_plane%d" % a0, [P, K_PASSES, n, SLOTS, P], U8) for a0, n in h_sorts.items()}
        a_rows = {piece: kept("a_rows%d_%d" % piece, [P, SLOTS, PASS], BF16) for piece in pieces}
        a_codes = {piece: kept("a_codes%d_%d" % piece, [P, PASS], U32) for piece in pieces}
        a_plane = {piece: kept("a_plane%d_%d" % piece, [P, PASS], U8) for piece in pieces}
        e_tiles = [(a, WIDE) for a in range(J_PASSES)] + [(0, NARROW), (2, NARROW)]
        e_rows = {tile: kept("e_rows%d_%d" % tile, [P, SLOTS, PASS], BF16) for tile in e_tiles}
        e_codes = {tile: kept("e_codes%d_%d" % tile, [P, PASS], U32) for tile in e_tiles}
        e_plane = {tile: kept("e_plane%d_%d" % tile, [P, PASS], U8) for tile in e_tiles}
        y_codes = [kept("y_codes%d" % g, [P, R], U32) for g in range(M_CHUNKS)]
        y_plane = [kept("y_plane%d" % n, [P, R], U8) for n in range(2)]

        def e_place(a, part):
            if part == WIDE:
                return (a, WIDE), 0
            return (a - a % 2, NARROW), (a % 2) * R_PARTS[NARROW][1]

        vector.memset(one[:], 1.0)
        vector.memset(h_plane_raw[:].rearrange("p g n -> p (g n)").bitcast(I32), 0)
        vector.memset(ident[:], 0.0)
        vector.memset(c_plane[:].rearrange("p g n -> p (g n)").bitcast(I32), 0)
        scalar.activation(out=ln_rows[:].rearrange("p t n -> p (t n)"), in_=one[:].to_broadcast([P, PASS]), func=ACT.Ln)
        make_identity(nc, ident[:], nomemset=True)

        def load_plane(plane, scales, quadrants):
            for q in quadrants:
                nc.sync.dma_start(
                    out=plane[32 * q : 32 * q + 4, :, :].bitcast(I32),
                    in_=scales[:, 4 * q : 4 * q + 4, :].rearrange("g r n -> r g n").bitcast(I32),
                )

        def load_piece(a, g):
            src = alleles[PASS * a : PASS * (a + 1), PASS * g : PASS * (g + 1)].rearrange("(s t i) m -> i s t m", t=SLOTS, i=4)
            for i in range(4):
                nc.sync.dma_start(out=a_rows[a, g][i:P:4, :, :], in_=src[i])

        def load_h(a0):
            cols = slice(2 * PASS * a0, 2 * PASS * (a0 + h_loads[a0]))
            nc.sync.dma_start(out=h_raw[a0][:].bitcast(I32), in_=h_words[:, :, cols].rearrange("g p n -> p g n").bitcast(I32))

        def load_c(part):
            r0, width = R_PARTS[part]
            cols = slice(2 * r0, 2 * (r0 + width))
            nc.sync.dma_start(out=c_codes[part][:].bitcast(I32), in_=c_words[:, :, cols].rearrange("g p n -> p g n").bitcast(I32))

        def load_gain(g):
            nc.sync.dma_start(out=gain[g][:], in_=marker_gain[PASS * g : PASS * (g + 1)].partition_broadcast(P))

        nc.sync.dma_start(out=vectors[0:J_PASSES, :], in_=hap_weight.rearrange("(a n) -> a n", n=PASS))
        load_piece(0, 0)
        load_plane(h_plane_raw, h_scales, (0,))
        load_h(0)
        load_c(WIDE)
        load_plane(h_plane_raw, h_scales, (1, 2, 3))
        load_plane(c_plane, c_scales, (0, 1, 2, 3))
        load_h(1)
        load_piece(1, 0)
        load_h(2)
        load_piece(2, 0)
        nc.sync.dma_start(out=vectors[SCALE_ROW:BASE_ROW, 0:P], in_=target_scale.rearrange("(a n) -> a n", n=P))
        nc.sync.dma_start(out=vectors[BASE_ROW:END_ROW, 0:P], in_=base.rearrange("(a n) -> a n", n=P))
        load_piece(3, 0)
        load_c(NARROW)
        load_gain(0)
        for g in range(1, M_CHUNKS):
            for a in range(J_PASSES):
                load_piece(a, g)
            load_gain(g)

        grouped = {}

        def interleave(engine, key, rows, cols, tag):
            if key not in grouped:
                bufs = 1 if tag == "for_gpsimd" else 3
                grouped[key] = work.tile([P, PASS, SLOTS], BF16, name=tag, tag=tag, bufs=bufs, align_bytes=64)
            dst, src = grouped[key][:, cols, :], rows[:, :, cols]
            if engine is gpsimd:
                gpsimd.tensor_scalar(
                    out=dst, in0=src.rearrange("p t c -> p c t"), scalar1=1.0, scalar2=-0.0, op0=ALU.mult, op1=ALU.add
                )
                return
            dst, src = dst.rearrange("p (c i) t -> p c t i", i=4), src.rearrange("p t (c i) -> p c t i", i=4)
            if engine is scalar:
                scalar.copy(out=dst, in_=src)
            else:
                vector.tensor_copy(out=dst, in_=src)

        def quantise(key, codes, plane):
            vector.quantize_mx(out=codes.bitcast(FP8X4), scales=plane, in_=grouped[key][:].rearrange("p c t -> p (c t)"))

        def group_a(engine, piece, tag, cols=slice(0, PASS)):
            interleave(engine, ("a", piece), a_rows[piece][:], cols, tag)

        def quantise_a(piece):
            quantise(("a", piece), a_codes[piece][:], a_plane[piece][:])

        def group_e(engine, tile, tag):
            interleave(engine, ("e", tile), e_rows[tile][:], slice(0, PASS), tag)

        def quantise_e(tile):
            quantise(("e", tile), e_codes[tile][:], e_plane[tile][:])

        def h_place(a, starts):
            a0 = max(start for start in starts if start <= a)
            return a0, a - a0

        def sort_h_words(a):
            a0, n = h_place(a, h_loads)
            vector.tensor_copy(
                out=h_codes[a0][:, n].bitcast(I32).rearrange("p g t (s e) -> p g t s e", e=2),
                in_=h_raw[a0][:, :, 2 * PASS * n : 2 * PASS * (n + 1)].bitcast(I32).rearrange("p g (s t e) -> p g t s e", t=SLOTS, e=2),
            )

        def sort_h_plane(a0):
            cols = slice(PASS * a0, PASS * (a0 + h_sorts[a0]))
            vector.tensor_copy(
                out=h_plane[a0][:].bitcast(I32),
                in_=h_plane_raw[:, :, cols].bitcast(I32).rearrange("p g (a s t) -> p g a t s", t=SLOTS, a=h_sorts[a0]),
            )

        def emission(a, part):
            r0, width = R_PARTS[part]
            tile, col0 = e_place(a, part)
            words0, words_n = h_place(a, h_loads)
            plane0, plane_n = h_place(a, h_sorts)
            for t in range(SLOTS):
                bank = mx_bank()
                for g in range(K_PASSES):
                    nc.tensor.matmul_mx(
                        out=bank[:, 0:width],
                        lhsT=h_codes[words0][:, words_n, g, t, :].bitcast(FP4X4),
                        lhsT_scale=h_plane[plane0][:, g, plane_n, t, :],
                        rhs=c_codes[part][:, g, :].bitcast(FP4X4),
                        rhs_scale=c_plane[:, g, r0 : r0 + width],
                        start=(g == 0),
                        stop=(g == K_PASSES - 1),
                    )
                scalar.activation(
                    out=e_rows[tile][:, t, col0 : col0 + width], in_=bank[:, 0:width], func=ACT.Exp, bias=ln_weight[:, t, a : a + 1]
                )

        base_bank, d_bank, z_of, y_of, rounded, turned, y_grouped = {}, {}, {}, {}, {}, {}, {}

        def place(pair, h):
            g, k = divmod(pair, PAIRS_PER_CHUNK)
            return g, 2 * k + h

        def product(pair, h, a):
            g, rt = place(pair, h)
            part = WIDE if P * rt < R_PARTS[NARROW][0] else NARROW
            if a == 0:
                d_bank[pair, h] = mx_bank()
            tile, col0 = e_place(a, part)
            first = col0 + P * rt - R_PARTS[part][0]
            nc.tensor.matmul_mx(
                out=d_bank[pair, h][:],
                lhsT=e_codes[tile][:, first : first + P].bitcast(FP8X4),
                lhsT_scale=e_plane[tile][:, first : first + P],
                rhs=a_codes[a, g][:].bitcast(FP8X4),
                rhs_scale=a_plane[a, g][:],
                start=(a == 0),
                stop=(a == J_PASSES - 1),
            )

        def scale_d(pair, h):
            g, rt = place(pair, h)
            if h == 0:
                z_of[pair] = work.tile([P, 2, PASS], F32, name="z", tag="z", bufs=2)
            vector.scalar_tensor_tensor(
                out=z_of[pair][:, h, :],
                in0=d_bank[pair, h][:],
                scalar=vec_cols[:, rt : rt + 1],
                in1=gain[g][:],
                op0=ALU.mult,
                op1=ALU.mult,
            )

        def spread_base(g):
            base_bank[g] = psum.tile([P, PASS], F32, name="base_bank", tag="base_bank", bufs=2)
            for c in range(PASS // P):
                col = R_TILES + (PASS // P) * g + c
                nc.tensor.transpose(base_bank[g][:, P * c : P * (c + 1)], vec_cols[:, col : col + 1].to_broadcast([P, P]), ident[:])

        def add_base(pair, h0, h1):
            if h0 == 0:
                y_of[pair] = work.tile([P, 2, PASS], F32, name="y", tag="y", bufs=4)
            g, rt = place(pair, h0)
            vector.tensor_tensor(
                out=y_of[pair][:, h0:h1, :],
                in0=z_of[pair][:, h0:h1, :],
                in1=base_bank[g][:].unsqueeze(1).to_broadcast([P, h1 - h0, PASS]),
                op=ALU.add,
            )
            dst = out_0[P * rt : P * (rt + h1 - h0), PASS * g : PASS * (g + 1)]
            nc.sync.dma_start(out=dst.rearrange("(h r) m -> r h m", r=P), in_=y_of[pair][:, h0:h1, :])

        def by_word(ap):
            return ap.rearrange("r (p u e) -> r u p e", u=2, e=2)

        def open_rounded(pair):
            rounded[pair] = work.tile([P, 2, 2, P, 2], BF16, name="rounded", tag="rounded", bufs=3, align_bytes=64)

        def round_y(pair):
            open_rounded(pair)
            scalar.copy(out=rounded[pair][:], in_=y_of[pair][:].rearrange("r h (p u e) -> r h u p e", u=2, e=2))

        def turn(pair):
            turned[pair] = turn_bank()
            words = rounded[pair][:].rearrange("r h u p e -> r (h u p e)").bitcast(F32)
            for c in range(PASS // P):
                nc.tensor.transpose(turned[pair][:, P * c : P * (c + 1)], words[:, P * c : P * (c + 1)], ident[:])

        def group_y(pair):
            y_grouped[pair] = work.tile([P, 2 * P * SLOTS], BF16, name="y_grouped", tag="y_grouped", bufs=4, align_bytes=64)
            scalar.copy(
                out=y_grouped[pair][:].bitcast(F32).rearrange("p (h r u) -> p h r u", h=2, u=2),
                in_=turned[pair][:].rearrange("p (h u r) -> p h r u", h=2, u=2),
            )

        def planes(pair):
            g, rt = place(pair, 0)
            cols = slice(P * rt, P * (rt + 2))
            plane = y_plane[min(g, 1)]
            vector.quantize_mx(out=y_codes[g][:, cols].bitcast(FP8X4), scales=plane[4 * max(g - 1, 0) : P, cols], in_=y_grouped[pair][:])
            nc.sync.dma_start(out=out_1[g, :, cols, :].rearrange("p m t -> p (m t)").bitcast(I32), in_=y_codes[g][:, cols].bitcast(I32))

        def store_plane(queue, plane, g0, g1):
            for q in range(4):
                queue.dma_start(
                    out=out_2[g0:g1, 4 * q : 4 * q + 4, :].bitcast(I32),
                    in_=plane[32 * q : 32 * q + 4 * (g1 - g0), :].bitcast(I32),
                )

        scalar.activation(
            out=ln_rows[0:J_PASSES, :, :].rearrange("a t (s i) -> a t s i", i=4),
            in_=vectors[0:J_PASSES, :].rearrange("a (s t i) -> a t s i", t=SLOTS, i=4),
            func=ACT.Ln,
        )
        scalar.activation(out=vec_rows[:], in_=one[:].to_broadcast([P, P]), func=ACT.Exp)
        group_a(vector, (0, 0), "for_vector")
        ln_bank = turn_bank()
        for t in range(SLOTS):
            nc.tensor.transpose(ln_bank[:, P * t : P * (t + 1)], ln_rows[:, t, :], ident[:])
        vector.tensor_copy(out=ln_weight[:], in_=ln_bank[:].rearrange("p (t n) -> p t n", t=SLOTS)[:, :, 0:J_PASSES])
        quantise_a((0, 0))
        sort_h_words(0)
        sort_h_plane(0)
        sort_h_plane(1)

        emission(0, WIDE)
        sort_h_words(1)
        group_a(vector, (1, 0), "for_vector")
        sort_h_words(2)
        quantise_a((1, 0))
        emission(1, WIDE)
        group_e(vector, (0, WIDE), "for_vector")
        sort_h_words(3)
        quantise_e((0, WIDE))
        emission(2, WIDE)
        group_a(vector, (2, 0), "for_vector")
        group_e(vector, (1, WIDE), "for_vector")
        vector.tensor_copy(out=vec_rows[SCALE_ROW:END_ROW, :], in_=vectors[SCALE_ROW:END_ROW, 0:P])
        quantise_a((2, 0))
        quantise_e((1, WIDE))
        emission(3, WIDE)
        vec_bank = turn_bank()
        nc.tensor.transpose(vec_bank[:, 0:P], vec_rows[:], ident[:])
        vector.tensor_copy(out=vec_cols[:], in_=vec_bank[:, SCALE_ROW:END_ROW])
        group_a(vector, (3, 0), "for_vector")
        group_e(vector, (2, WIDE), "for_vector")
        quantise_a((3, 0))

        emission(0, NARROW)
        spread_base(0)
        emission(1, NARROW)
        group_e(vector, (3, WIDE), "for_vector")
        quantise_e((2, WIDE))
        emission(2, NARROW)
        emission(3, NARROW)
        quantise_e((3, WIDE))
        group_e(vector, (0, NARROW), "for_gpsimd")

        later = [(a, g) for g in range(1, M_CHUNKS) for a in range(J_PASSES)]
        quantised = 0

        def start_gpsimd(pair):
            group_a(gpsimd, GPSIMD_PIECES[pair], "for_gpsimd", slice(0, GPSIMD_COLS))

        for pair in range(LAST):
            for a in range(J_PASSES):
                product(pair, 0, a)
                product(pair, 1, a)
            scale_d(pair, 0)
            if pair == 0:
                quantise_e((0, NARROW))
                start_gpsimd(0)
            scale_d(pair, 1)
            if pair >= 2:
                turn(pair - 2)
            if pair in (2, 4):
                spread_base(pair // 2)

            if pair == 0:
                group_e(scalar, (2, NARROW), "for_scalar")
                group_a(scalar, later[0], "for_scalar")
            elif pair <= len(GPSIMD_PIECES):
                group_a(scalar, GPSIMD_PIECES[pair - 1], "for_gpsimd", slice(GPSIMD_COLS, PASS))
            if pair >= 1:
                round_y(pair - 1)
            if pair >= 2:
                group_y(pair - 2)
            if 1 <= pair < len(GPSIMD_PIECES):
                between = later[later.index(GPSIMD_PIECES[pair - 1]) + 1 : later.index(GPSIMD_PIECES[pair])]
                for piece in between:
                    group_a(scalar, piece, "for_scalar")

            if pair >= 3:
                planes(pair - 3)
            if pair - 3 == PAIRS_PER_CHUNK - 1:
                store_plane(nc.sync, y_plane[0], 0, 1)
            if pair == 1:
                quantise_e((2, NARROW))
            if 1 <= pair <= len(GPSIMD_PIECES):
                due = later.index(GPSIMD_PIECES[pair - 1]) + 1
                for piece in later[quantised:due]:
                    quantise_a(piece)
                quantised = due
            if 1 <= pair < len(GPSIMD_PIECES):
                start_gpsimd(pair)
            add_base(pair, 0, 2)

        for h in range(2):
            for a in range(J_PASSES):
                product(LAST, h, a)
        scale_d(LAST, 0)
        planes(LAST - 3)
        add_base(LAST, 0, 1)
        open_rounded(LAST)
        gpsimd.tensor_scalar(
            out=rounded[LAST][:, 0], in0=by_word(y_of[LAST][:, 0, :]), scalar1=1.0, scalar2=-0.0, op0=ALU.mult, op1=ALU.add
        )
        scale_d(LAST, 1)
        turn(LAST - 2)
        round_y(LAST - 1)
        group_y(LAST - 2)
        vector.tensor_tensor(
            out=rounded[LAST][:, 1], in0=by_word(z_of[LAST][:, 1, :]), in1=by_word(base_bank[M_CHUNKS - 1][:]), op=ALU.add
        )
        add_base(LAST, 1, 2)
        planes(LAST - 2)
        for pair in (LAST - 1, LAST):
            turn(pair)
            group_y(pair)
        for pair in (LAST - 1, LAST):
            planes(pair)
        store_plane(scalar, y_plane[1], 1, M_CHUNKS)
